import numpy as np
import ml_dtypes


def mxq(x, axis, fmt="e4m3"):
    dtype, down = {"e4m3": (ml_dtypes.float8_e4m3fn, 7), "e5m2": (ml_dtypes.float8_e5m2, 14)}[fmt]
    v = np.moveaxis(np.asarray(x, np.float32).astype(ml_dtypes.bfloat16).astype(np.float64), axis, -1)
    blocks = v.reshape(v.shape[:-1] + (-1, 32))
    amax = np.abs(blocks).max(-1, keepdims=True)
    byte = np.maximum(np.where(amax > 0, np.frexp(amax)[1] - 1 + 127, 0) - down, 1)
    scale = np.exp2(byte - 127.0)
    codes = (blocks / scale).astype(np.float32).astype(dtype).astype(np.float64)
    return np.moveaxis((codes * scale).reshape(v.shape), -1, axis)


WIDE = False


def mx_kscale(k):
    if not WIDE:
        return np.ones(k)
    levels = np.array([10, -10, 5, -5, 0])
    if k % 512:
        return np.exp2(np.random.permutation(np.resize(levels, k // 32))).repeat(32)
    a = np.empty((k // 512, 16))
    for p in range(k // 512):
        a[p, :8] = np.random.permutation(np.resize(levels, 8))
        for g in range(8):
            far = levels[np.abs(levels - a[p, g]) >= 10]
            a[p, g + 8] = far[np.random.randint(len(far))]
    return np.exp2(a.ravel()).repeat(32)


def f64(x):
    return np.asarray(x).astype(np.float64)


def striped(idx):
    return np.tile(idx.reshape(-1, 16).T, (8, 1)).astype(np.uint16)


def unstriped(offs):
    return offs[:16].T.reshape(-1).astype(np.int64)


E2M1 = np.array([0.0, 0.5, 1.0, 1.5, 2.0, 3.0, 4.0, 6.0, -0.0, -0.5, -1.0, -1.5, -2.0, -3.0, -4.0, -6.0])


def pack_weight(w, fmt):
    k, n = w.shape
    w = f64(np.asarray(w, np.float32).astype(ml_dtypes.bfloat16)).reshape(k // 32, 32, n)
    amax = np.abs(w).max(1)
    if fmt == "e4m3":
        byte = np.frexp(amax)[1] - 1 + 127 - 7
    else:
        mant, ex = np.frexp(amax / 6.0)
        byte = np.where(mant > 0.5, ex, ex - 1) + 127
    byte = np.clip(np.where(amax > 0, byte, 1), 1, 254)
    scaled = (w * np.exp2(127.0 - byte)[:, None, :]).reshape(k, n).astype(np.float32)
    by_word = np.ascontiguousarray(scaled.reshape(k // 512, 128, 4, n).transpose(0, 1, 3, 2))
    if fmt == "e4m3":
        words = by_word.astype(ml_dtypes.float8_e4m3fn).view(np.uint8)
    else:
        c = by_word.astype(ml_dtypes.float4_e2m1fn).view(np.uint8) & 0xF
        words = (c[..., 0::2] | (c[..., 1::2] << 4)).reshape(k // 512, 128, 2 * n)
    return np.ascontiguousarray(words), np.ascontiguousarray(byte.astype(np.uint8).reshape(k // 512, 16, n))


def unpack_weight(words, scales, fmt):
    g, _, n = scales.shape
    words = np.ascontiguousarray(words).reshape(g, 128, n, -1)
    if fmt == "e4m3":
        vals = words.view(ml_dtypes.float8_e4m3fn).astype(np.float64)
    else:
        nib = np.empty((g, 128, n, 4), np.uint8)
        nib[..., 0::2] = words & 0xF
        nib[..., 1::2] = words >> 4
        vals = E2M1[nib]
    vals = vals * np.repeat(np.exp2(scales.astype(np.float64) - 127.0), 8, axis=1)[..., None]
    return vals.transpose(0, 1, 3, 2).reshape(g * 512, n)


def gelu(v):
    return 0.5 * v * (1.0 + np.tanh(np.sqrt(2.0 / np.pi) * (v + 0.044715 * v**3)))


K, T, E, C, N = 1024, 1536, 12, 256, 128
K8 = 512


def by_expert(wq, xq):
    return np.concatenate([wq[e].T @ xq[:, e * C:(e + 1) * C] for e in range(E)], axis=1)


def setup_inputs():
    n = np.random.standard_normal
    s = mx_kscale(K)[:, None]
    first = np.random.permutation(np.repeat(np.arange(E), T // E))
    second = (first + 1 + np.random.permutation(np.repeat(np.arange(E - 1), -(-T // (E - 1)))[:T])) % E
    while np.bincount(second, minlength=E).max() != T // E:
        load = np.bincount(second, minlength=E); hi, lo = int(load.argmax()), int(load.argmin())
        t = np.flatnonzero((second == hi) & (first != lo))[0]; second[t] = lo
    slot_token = np.empty(E * C, np.int64); pos = np.empty((2, T), np.int64); fill = np.zeros(E, np.int64)
    place = np.stack([np.random.permutation(C) for _ in range(E)])
    for r, deal in enumerate((first, second)):
        for t in np.random.permutation(T):
            e = deal[t]; j = e * C + place[e, fill[e]]; fill[e] += 1; slot_token[j] = t; pos[r, t] = j
    g = np.random.uniform(0.2, 0.8, T)
    w = n((E, K, N)) / np.sqrt(K) / s[None]
    w8 = [pack_weight(m[:K8], "e4m3") for m in w]
    w4 = [pack_weight(m[K8:], "e2m1") for m in w]
    return {
        "xT": (n((K, T)) * s).astype(np.float32),
        "w8_words": np.stack([m[0] for m in w8]),
        "w8_scales": np.stack([m[1] for m in w8]),
        "w4_words": np.stack([m[0] for m in w4]),
        "w4_scales": np.stack([m[1] for m in w4]),
        "b": (0.3 * n((N, E))).astype(np.float32),
        "gate": np.stack([np.tile(g, (N, 1)), np.tile(1.0 - g, (N, 1))]).astype(np.float32),
        "offs": striped(slot_token),
        "pos1": striped(pos[0]),
        "pos2": striped(pos[1]),
    }


def reference(xT, w8_words, w8_scales, w4_words, w4_scales, b, gate, offs, pos1, pos2):
    idx = unstriped(offs)
    w = np.stack([np.concatenate([unpack_weight(w8_words[e], w8_scales[e], "e4m3"), unpack_weight(w4_words[e], w4_scales[e], "e2m1")]) for e in range(E)])
    xq = mxq(f64(xT)[:, idx], 0, "e4m3")
    y = by_expert(w, xq)
    y = gelu(y + np.repeat(f64(b), C, axis=1))
    return f64(gate[0]) * y[:, unstriped(pos1)] + f64(gate[1]) * y[:, unstriped(pos2)]

@@ -1,0 +1,233 @@
+from contextlib import ExitStack
+
+import concourse.mybir as mybir
+
+K, T, E, C, N = 1024, 1536, 12, 256, 128
+S = E * C
+FLOPS = 2 * S * K * N
+
+P = 128
+PACK = 4
+K_PASS = P * PACK
+GROUP = 128
+
+F32 = mybir.dt.float32
+BF16 = mybir.dt.bfloat16
+I32 = mybir.dt.int32
+U32 = mybir.dt.uint32
+U16 = mybir.dt.uint16
+U8 = mybir.dt.uint8
+FP8X4 = mybir.dt.float8_e4m3fn_x4
+FP4X4 = mybir.dt.float4_e2m1fn_x4
+ACT = mybir.ActivationFunctionType
+MULT, ADD = mybir.AluOpType.mult, mybir.AluOpType.add
+
+CHUNKS = (
+    ((0, 768, 384), (768, 512, 256), (1280, 256, 160)),
+    ((0, 256, 0), (256, 512, 0), (768, 512, 0), (1280, 256, 128)),
+)
+SCALE_ROW = (4, 0)
+
+
+def tile_moe_pln_lin_gelu_kernel(
+    tc, xT, w8_words, w8_scales, w4_words, w4_scales, b, gate, offs, pos1, pos2, out
+):
+    nc = tc.nc
+    with ExitStack() as ctx:
+        lists = ctx.enter_context(tc.tile_pool(name="lists", bufs=1))
+        keep = ctx.enter_context(tc.tile_pool(name="keep", bufs=1))
+        psum = ctx.enter_context(tc.psum_pool(name="psum", bufs=1))
+
+        offs_sb = lists.tile([P, S // 16], U16, name="offs_sb")
+        pos1_sb = lists.tile([P, T // 16], U16, name="pos1_sb")
+        pos2_sb = lists.tile([P, T // 16], U16, name="pos2_sb")
+
+        x_words = [keep.tile([P, T], U32, name=f"x_words{a}", align_bytes=64) for a in range(2)]
+        x_scales = keep.tile([P, T], U8, name="x_scales", align_bytes=64)
+        slot_words = [keep.tile([P, S], U32, name=f"slot_words{a}", align_bytes=64) for a in range(2)]
+        slot_scales = keep.tile([P, S], U8, name="slot_scales", align_bytes=64)
+        w8_sb = keep.tile([P, E * N * 4], U8, name="w8_sb", align_bytes=64)
+        w4_sb = keep.tile([P, E * N * 2], U8, name="w4_sb", align_bytes=64)
+        w8_planes = keep.tile([P, E * N], U8, name="w8_planes", align_bytes=64)
+        w4_planes = keep.tile([P, E * N], U8, name="w4_planes", align_bytes=64)
+        bias = keep.tile([P, E], F32, name="bias")
+        gates = [keep.tile([P, T], F32, name=f"gate{r}") for r in range(2)]
+        y = keep.tile([P, S], F32, name="y")
+        warm = keep.tile([P, 1], F32, name="warm")
+
+        nc.gpsimd.memset(x_scales[:], 0)
+        nc.vector.memset(warm[:], 0.0)
+        nc.vector.memset(w8_planes[:].bitcast(I32), 0)
+        nc.vector.memset(w4_planes[:].bitcast(I32), 0)
+        nc.scalar.activation(warm[:], warm[:], ACT.Gelu_apprx_tanh)
+
+        raw = {}
+
+        def load_chunk(a, c):
+            t0, width, _ = CHUNKS[a][c]
+            tile = keep.tile([P, PACK, width], F32, name=f"raw{a}_{c}")
+            rows = xT[a * K_PASS : (a + 1) * K_PASS, t0 : t0 + width]
+            nc.sync.dma_start(out=tile[:], in_=rows.rearrange("(p j) w -> p j w", j=PACK))
+            raw[a, c] = tile
+
+        for c in range(3):
+            load_chunk(0, c)
+        nc.sync.dma_start(offs_sb[:], offs)
+        for c in range(4):
+            load_chunk(1, c)
+
+        for planes, scales in ((w8_planes, w8_scales), (w4_planes, w4_scales)):
+            for q in range(4):
+                nc.sync.dma_start(
+                    out=planes[32 * q : 32 * q + 4, :].bitcast(I32).rearrange("q (e n) -> q e n", e=E),
+                    in_=scales[:, 0, 4 * q : 4 * q + 4, :].bitcast(I32).rearrange("e q n -> q e n"),
+                )
+        nc.sync.dma_start(bias[:], b)
+        half = E // 2
+        for h in range(2):
+            experts = slice(h * half, (h + 1) * half)
+            nc.sync.dma_start(
+                out=w8_sb[:, h * half * N * 4 : (h + 1) * half * N * 4].bitcast(I32).rearrange("p (e n) -> p e n", e=half),
+                in_=w8_words[experts, 0].rearrange("e p n r -> e p (n r)").bitcast(I32).rearrange("e p n -> p e n"),
+            )
+            nc.sync.dma_start(
+                out=w4_sb[:, h * half * N * 2 : (h + 1) * half * N * 2].bitcast(I32).rearrange("p (e n) -> p e n", e=half),
+                in_=w4_words[experts, 0].bitcast(I32).rearrange("e p n -> p e n"),
+            )
+        nc.sync.dma_start(pos1_sb[:], pos1)
+        nc.sync.dma_start(pos2_sb[:], pos2)
+        for r in range(2):
+            nc.sync.dma_start(gates[r][:], gate[r])
+
+        grouped = {}
+
+        def interleave(a, c):
+            _, width, by_vector = CHUNKS[a][c]
+            tile = keep.tile([P, width, PACK], BF16, name=f"grouped{a}_{c}", align_bytes=64)
+            grouped[a, c] = tile
+
+            def views(lo, hi):
+                dst = tile[:, lo:hi, :].rearrange("p (c i) t -> p c t i", i=4)
+                src = raw[a, c][:, :, lo:hi].rearrange("p t (c i) -> p c t i", i=4)
+                return dst, src
+
+            if by_vector < width:
+                dst, src = views(by_vector, width)
+                nc.scalar.activation(dst, src, ACT.Copy)
+            if by_vector > 0:
+                dst, src = views(0, by_vector)
+                nc.vector.tensor_copy(dst, src)
+
+        def quantise(a, c):
+            t0, width, _ = CHUNKS[a][c]
+            for lo in range(0, width, 512):
+                hi = min(width, lo + 512)
+                nc.vector.quantize_mx(
+                    out=x_words[a][:, t0 + lo : t0 + hi].bitcast(FP8X4),
+                    scales=x_scales[SCALE_ROW[a] : P, t0 + lo : t0 + hi],
+                    in_=grouped[a, c][:, lo:hi, :].rearrange("p w j -> p (w j)"),
+                )
+
+        def gather(dst, window, lo, hi):
+            nc.vector.tensor_copy(dst[:, lo:hi], window[:].indirect(offs_sb[:, lo // 16 : hi // 16]))
+
+        for c in range(3):
+            interleave(0, c)
+            quantise(0, c)
+        for c in range(3):
+            interleave(1, c)
+        gather(slot_words[0], x_words[0], 0, 1024)
+        gather(slot_words[0], x_words[0], 1024, 2048)
+        gather(slot_words[0], x_words[0], 2048, 3072)
+        quantise(1, 0)
+        quantise(1, 1)
+        interleave(1, 3)
+        quantise(1, 2)
+        quantise(1, 3)
+
+        banks = {}
+
+        def first_pass(e, g):
+            bank = banks[e, g]
+            cols = slice(e * C + g * GROUP, e * C + (g + 1) * GROUP)
+            nc.tensor.matmul_mx(
+                out=bank,
+                lhsT=w8_sb[:, e * N * 4 : (e + 1) * N * 4].bitcast(FP8X4),
+                lhsT_scale=w8_planes[:, e * N : (e + 1) * N],
+                rhs=slot_words[0][:, cols].bitcast(FP8X4),
+                rhs_scale=slot_scales[SCALE_ROW[0] : P, cols],
+                start=True,
+                stop=False,
+            )
+
+        def second_pass(e, g):
+            bank = banks[e, g]
+            cols = slice(e * C + g * GROUP, e * C + (g + 1) * GROUP)
+            nc.tensor.matmul_mx(
+                out=bank,
+                lhsT=w4_sb[:, e * N * 2 : (e + 1) * N * 2].bitcast(FP4X4),
+                lhsT_scale=w4_planes[:, e * N : (e + 1) * N],
+                rhs=slot_words[1][:, cols].bitcast(FP8X4),
+                rhs_scale=slot_scales[SCALE_ROW[1] : P, cols],
+                start=False,
+                stop=True,
+            )
+
+        def gelu(e, bank, lo, hi):
+            nc.scalar.activation(y[:, lo:hi], bank, ACT.Gelu_apprx_tanh, bias=bias[:, e : e + 1])
+
+        last = E - 1
+        tail_banks = [psum.tile([P, GROUP], F32, name=f"tail{g}") for g in range(2)]
+        for g in range(2):
+            banks[last, g] = tail_banks[g][:]
+
+        def expert(e):
+            bank = psum.tile([P, C], F32, name=f"bank{e % 6}")
+            for g in range(2):
+                banks[e, g] = bank[:, g * GROUP : (g + 1) * GROUP]
+                first_pass(e, g)
+                second_pass(e, g)
+            gelu(e, bank[:], e * C, (e + 1) * C)
+
+        for lo in range(0, S, 1024):
+            gather(slot_scales, x_scales, lo, lo + 1024)
+            if lo == 2048:
+                for g in range(2):
+                    first_pass(last, g)
+                cuts = (2048, 2560, 2816)
+            else:
+                cuts = (lo, lo + 1024)
+            for a0, a1 in zip(cuts[:-1], cuts[1:]):
+                gather(slot_words[1], x_words[1], a0, a1)
+                for e in range(a0 // C, a1 // C):
+                    expert(e)
+        gather(slot_words[1], x_words[1], 2816, 3072)
+        for g in range(2):
+            second_pass(last, g)
+            gelu(last, banks[last, g], last * C + g * GROUP, last * C + (g + 1) * GROUP)
+
+        pieces = ((0, 704), (704, 1408), (1408, 1536))
+        picked = {}
+
+        def pick(r, i):
+            lo, hi = pieces[i]
+            pos = (pos1_sb, pos2_sb)[r]
+            tile = keep.tile([P, hi - lo], F32, name=f"picked{r}_{i}")
+            nc.vector.tensor_tensor(tile[:], y[:].indirect(pos[:, lo // 16 : hi // 16]), gates[r][:, lo:hi], MULT)
+            picked[r, i] = tile
+
+        def combine(i):
+            lo, hi = pieces[i]
+            total = keep.tile([P, hi - lo], F32, name=f"total{i}")
+            nc.vector.tensor_tensor(total[:], picked[0, i][:], picked[1, i][:], ADD)
+            nc.sync.dma_start(out[:, lo:hi], total[:])
+
+        pick(0, 0)
+        pick(1, 0)
+        pick(0, 1)
+        combine(0)
+        pick(1, 1)
+        pick(0, 2)
+        combine(1)
+        pick(1, 2)
+        combine(2)

@@ -1,6 +1,7 @@
 from contextlib import ExitStack
 
 import concourse.mybir as mybir
+from concourse.masks import make_identity
 
 K, T, E, C, N = 1024, 1536, 12, 256, 128
 S = E * C
@@ -22,9 +23,9 @@ FP4X4 = mybir.dt.float4_e2m1fn_x4
 ACT = mybir.ActivationFunctionType
 MULT, ADD = mybir.AluOpType.mult, mybir.AluOpType.add
 
-CHUNKS = (
-    ((0, 768, 384), (768, 512, 256), (1280, 256, 160)),
-    ((0, 256, 0), (256, 512, 0), (768, 512, 0), (1280, 256, 128)),
+LOADS = (
+    ((768, 384), (512, 256), (256, 160)),
+    ((256, 0), (512, 0), (512, 0), (256, 128)),
 )
 SCALE_ROW = (4, 0)
 
@@ -51,11 +52,14 @@ def tile_moe_pln_lin_gelu_kernel(
         w8_planes = keep.tile([P, E * N], U8, name="w8_planes", align_bytes=64)
         w4_planes = keep.tile([P, E * N], U8, name="w4_planes", align_bytes=64)
         bias = keep.tile([P, E], F32, name="bias")
-        gates = [keep.tile([P, T], F32, name=f"gate{r}") for r in range(2)]
+        gates = keep.tile([P, 2, T], F32, name="gates")
         y = keep.tile([P, S], F32, name="y")
         warm = keep.tile([P, 1], F32, name="warm")
 
+        identity = keep.tile([P, P], F32, name="identity")
+
         nc.gpsimd.memset(x_scales[:], 0)
+        make_identity(nc, identity[:])
         nc.vector.memset(warm[:], 0.0)
         nc.vector.memset(w8_planes[:].bitcast(I32), 0)
         nc.vector.memset(w4_planes[:].bitcast(I32), 0)
@@ -63,17 +67,21 @@ def tile_moe_pln_lin_gelu_kernel(
 
         raw = {}
 
+        def first_token(widths, c):
+            return sum(widths[:c])
+
         def load_chunk(a, c):
-            t0, width, _ = CHUNKS[a][c]
+            width = LOADS[a][c][0]
+            t0 = first_token([w for w, v in LOADS[a]], c)
             tile = keep.tile([P, PACK, width], F32, name=f"raw{a}_{c}")
             rows = xT[a * K_PASS : (a + 1) * K_PASS, t0 : t0 + width]
             nc.sync.dma_start(out=tile[:], in_=rows.rearrange("(p j) w -> p j w", j=PACK))
             raw[a, c] = tile
 
-        for c in range(3):
+        for c in range(len(LOADS[0])):
             load_chunk(0, c)
         nc.sync.dma_start(offs_sb[:], offs)
-        for c in range(4):
+        for c in range(len(LOADS[1])):
             load_chunk(1, c)
 
         for planes, scales in ((w8_planes, w8_scales), (w4_planes, w4_scales)):
@@ -96,19 +104,18 @@ def tile_moe_pln_lin_gelu_kernel(
             )
         nc.sync.dma_start(pos1_sb[:], pos1)
         nc.sync.dma_start(pos2_sb[:], pos2)
-        for r in range(2):
-            nc.sync.dma_start(gates[r][:], gate[r])
+        nc.sync.dma_start(gates[:], gate.rearrange("r p t -> p r t"))
 
         grouped = {}
 
         def interleave(a, c):
-            _, width, by_vector = CHUNKS[a][c]
+            width, by_vector = LOADS[a][c]
             tile = keep.tile([P, width, PACK], BF16, name=f"grouped{a}_{c}", align_bytes=64)
             grouped[a, c] = tile
 
             def views(lo, hi):
-                dst = tile[:, lo:hi, :].rearrange("p (c i) t -> p c t i", i=4)
-                src = raw[a, c][:, :, lo:hi].rearrange("p t (c i) -> p c t i", i=4)
+                dst = tile[:, lo:hi, :].rearrange("p (c i) t -> p c t i", i=2)
+                src = raw[a, c][:, :, lo:hi].rearrange("p t (c i) -> p c t i", i=2)
                 return dst, src
 
             if by_vector < width:
@@ -119,7 +126,8 @@ def tile_moe_pln_lin_gelu_kernel(
                 nc.vector.tensor_copy(dst, src)
 
         def quantise(a, c):
-            t0, width, _ = CHUNKS[a][c]
+            width = LOADS[a][c][0]
+            t0 = first_token([w for w, v in LOADS[a]], c)
             for lo in range(0, width, 512):
                 hi = min(width, lo + 512)
                 nc.vector.quantize_mx(
@@ -206,14 +214,14 @@ def tile_moe_pln_lin_gelu_kernel(
             second_pass(last, g)
             gelu(last, banks[last, g], last * C + g * GROUP, last * C + (g + 1) * GROUP)
 
-        pieces = ((0, 704), (704, 1408), (1408, 1536))
+        pieces = ((0, 256), (256, 512), (512, 768), (768, 1024), (1024, 1408), (1408, 1536))
         picked = {}
 
         def pick(r, i):
             lo, hi = pieces[i]
             pos = (pos1_sb, pos2_sb)[r]
             tile = keep.tile([P, hi - lo], F32, name=f"picked{r}_{i}")
-            nc.vector.tensor_tensor(tile[:], y[:].indirect(pos[:, lo // 16 : hi // 16]), gates[r][:, lo:hi], MULT)
+            nc.vector.tensor_tensor(tile[:], y[:].indirect(pos[:, lo // 16 : hi // 16]), gates[:, r, lo:hi], MULT)
             picked[r, i] = tile
 
         def combine(i):
@@ -222,12 +230,47 @@ def tile_moe_pln_lin_gelu_kernel(
             nc.vector.tensor_tensor(total[:], picked[0, i][:], picked[1, i][:], ADD)
             nc.sync.dma_start(out[:, lo:hi], total[:])
 
-        pick(0, 0)
-        pick(1, 0)
-        pick(0, 1)
-        combine(0)
-        pick(1, 1)
-        pick(0, 2)
-        combine(1)
-        pick(1, 2)
-        combine(2)
+        turned_sb = {}
+
+        def blocks(i):
+            lo, hi = pieces[i]
+            return [slice(c, c + P) for c in range(0, hi - lo, P)]
+
+        def turn_and_add(i):
+            lo, hi = pieces[i]
+            turned = psum.tile([P, hi - lo], F32, name=f"bank{i % 2}")
+            for block in blocks(i):
+                for r in range(2):
+                    nc.tensor.matmul(
+                        turned[:, block],
+                        lhsT=picked[r, i][:, block],
+                        rhs=identity[:],
+                        start=(r == 0),
+                        stop=(r == 1),
+                        is_transpose=True,
+                    )
+            turned_sb[i] = keep.tile([P, hi - lo], F32, name=f"turned{i}")
+            nc.scalar.copy(turned_sb[i][:], turned[:])
+
+        def turn_back(i):
+            lo, hi = pieces[i]
+            back = psum.tile([P, hi - lo], F32, name=f"bank{2 + i}")
+            for block in blocks(i):
+                nc.tensor.transpose(back[:, block], turned_sb[i][:, block], identity[:])
+            total = keep.tile([P, hi - lo], F32, name=f"total{i}")
+            nc.scalar.copy(total[:], back[:])
+            nc.scalar.dma_start(out[:, lo:hi], total[:])
+
+        for i in range(4):
+            pick(0, i)
+            pick(1, i)
+            turn_and_add(i)
+            if i > 0:
+                turn_back(i - 1)
+        turn_back(3)
+        pick(0, 4)
+        pick(1, 4)
+        pick(0, 5)
+        combine(4)
+        pick(1, 5)
+        combine(5)

@@ -24,9 +24,10 @@ ACT = mybir.ActivationFunctionType
 MULT, ADD = mybir.AluOpType.mult, mybir.AluOpType.add
 
 LOADS = (
-    ((768, 384), (512, 256), (256, 160)),
+    ((768, 512), (512, 256), (256, 160)),
     ((256, 0), (512, 0), (512, 0), (256, 128)),
 )
+QUANTS = (((512, 256), (256, 256), (256,)), ((256,), (512,), (512,), (256,)))
 SCALE_ROW = (4, 0)
 
 
@@ -95,12 +96,12 @@ def tile_moe_pln_lin_gelu_kernel(
         for h in range(2):
             experts = slice(h * half, (h + 1) * half)
             nc.sync.dma_start(
-                out=w8_sb[:, h * half * N * 4 : (h + 1) * half * N * 4].bitcast(I32).rearrange("p (e n) -> p e n", e=half),
-                in_=w8_words[experts, 0].rearrange("e p n r -> e p (n r)").bitcast(I32).rearrange("e p n -> p e n"),
-            )
-            nc.sync.dma_start(
                 out=w4_sb[:, h * half * N * 2 : (h + 1) * half * N * 2].bitcast(I32).rearrange("p (e n) -> p e n", e=half),
                 in_=w4_words[experts, 0].bitcast(I32).rearrange("e p n -> p e n"),
+            )
+            nc.sync.dma_start(
+                out=w8_sb[:, h * half * N * 4 : (h + 1) * half * N * 4].bitcast(I32).rearrange("p (e n) -> p e n", e=half),
+                in_=w8_words[experts, 0].rearrange("e p n r -> e p (n r)").bitcast(I32).rearrange("e p n -> p e n"),
             )
         nc.sync.dma_start(pos1_sb[:], pos1)
         nc.sync.dma_start(pos2_sb[:], pos2)
@@ -126,10 +127,10 @@ def tile_moe_pln_lin_gelu_kernel(
                 nc.vector.tensor_copy(dst, src)
 
         def quantise(a, c):
-            width = LOADS[a][c][0]
             t0 = first_token([w for w, v in LOADS[a]], c)
-            for lo in range(0, width, 512):
-                hi = min(width, lo + 512)
+            for q, width in enumerate(QUANTS[a][c]):
+                lo = first_token(QUANTS[a][c], q)
+                hi = lo + width
                 nc.vector.quantize_mx(
                     out=x_words[a][:, t0 + lo : t0 + hi].bitcast(FP8X4),
                     scales=x_scales[SCALE_ROW[a] : P, t0 + lo : t0 + hi],
@@ -189,20 +190,29 @@ def tile_moe_pln_lin_gelu_kernel(
         for g in range(2):
             banks[last, g] = tail_banks[g][:]
 
-        def expert(e):
+        def open_bank(e):
             bank = psum.tile([P, C], F32, name=f"bank{e % 6}")
+            banks[e] = bank
             for g in range(2):
                 banks[e, g] = bank[:, g * GROUP : (g + 1) * GROUP]
-                first_pass(e, g)
-                second_pass(e, g)
-            gelu(e, bank[:], e * C, (e + 1) * C)
+            first_pass(e, 0)
+
+        def expert(e):
+            if e not in banks:
+                open_bank(e)
+            second_pass(e, 0)
+            first_pass(e, 1)
+            second_pass(e, 1)
+            gelu(e, banks[e][:], e * C, (e + 1) * C)
 
         for lo in range(0, S, 1024):
             gather(slot_scales, x_scales, lo, lo + 1024)
             if lo == 2048:
+                for e in range(lo // C, last):
+                    open_bank(e)
                 for g in range(2):
                     first_pass(last, g)
-                cuts = (2048, 2560, 2816)
+                cuts = (2048, 2304, 2560, 2816)
             else:
                 cuts = (lo, lo + 1024)
             for a0, a1 in zip(cuts[:-1], cuts[1:]):
@@ -214,7 +224,7 @@ def tile_moe_pln_lin_gelu_kernel(
             second_pass(last, g)
             gelu(last, banks[last, g], last * C + g * GROUP, last * C + (g + 1) * GROUP)
 
-        pieces = ((0, 256), (256, 512), (512, 768), (768, 1024), (1024, 1408), (1408, 1536))
+        pieces = ((0, 384), (384, 640), (640, 896), (896, 1152), (1152, 1408), (1408, 1536))
         picked = {}
 
         def pick(r, i):

@@ -11,6 +11,8 @@ P = 128
 PACK = 4
 K_PASS = P * PACK
 GROUP = 128
+THIRD = S // 3
+EXPERT_BANKS = 6
 
 F32 = mybir.dt.float32
 BF16 = mybir.dt.bfloat16
@@ -25,10 +27,12 @@ MULT, ADD = mybir.AluOpType.mult, mybir.AluOpType.add
 
 LOADS = (
     ((768, 512), (512, 256), (256, 160)),
-    ((256, 0), (512, 0), (512, 0), (256, 128)),
+    ((256, 0), (384, 0), (512, 0), (384, 128)),
 )
-QUANTS = (((512, 256), (256, 256), (256,)), ((256,), (512,), (512,), (256,)))
+QUANTS = (((512, 256), (256, 256), (256,)), ((256,), (256, 128), (512,), (256, 128)))
 SCALE_ROW = (4, 0)
+TENSOR_PIECES = ((0, 384), (384, 640), (640, 896), (896, 1152))
+VECTOR_PIECES = ((1152, 1408), (1408, 1536))
 
 
 def tile_moe_pln_lin_gelu_kernel(
@@ -50,46 +54,40 @@ def tile_moe_pln_lin_gelu_kernel(
         slot_scales = keep.tile([P, S], U8, name="slot_scales", align_bytes=64)
         w8_sb = keep.tile([P, E * N * 4], U8, name="w8_sb", align_bytes=64)
         w4_sb = keep.tile([P, E * N * 2], U8, name="w4_sb", align_bytes=64)
-        w8_planes = keep.tile([P, E * N], U8, name="w8_planes", align_bytes=64)
-        w4_planes = keep.tile([P, E * N], U8, name="w4_planes", align_bytes=64)
+        w8_scales_sb = keep.tile([P, E * N], U8, name="w8_scales_sb", align_bytes=64)
+        w4_scales_sb = keep.tile([P, E * N], U8, name="w4_scales_sb", align_bytes=64)
         bias = keep.tile([P, E], F32, name="bias")
         gates = keep.tile([P, 2, T], F32, name="gates")
         y = keep.tile([P, S], F32, name="y")
-        warm = keep.tile([P, 1], F32, name="warm")
-
         identity = keep.tile([P, P], F32, name="identity")
 
         nc.gpsimd.memset(x_scales[:], 0)
         make_identity(nc, identity[:])
-        nc.vector.memset(warm[:], 0.0)
-        nc.vector.memset(w8_planes[:].bitcast(I32), 0)
-        nc.vector.memset(w4_planes[:].bitcast(I32), 0)
-        nc.scalar.activation(warm[:], warm[:], ACT.Gelu_apprx_tanh)
+        nc.vector.memset(w8_scales_sb[:].bitcast(I32), 0)
+        nc.vector.memset(w4_scales_sb[:].bitcast(I32), 0)
 
         raw = {}
 
-        def first_token(widths, c):
-            return sum(widths[:c])
+        def first_token(a, c):
+            return sum(tokens for tokens, by_vector in LOADS[a][:c])
 
-        def load_chunk(a, c):
-            width = LOADS[a][c][0]
-            t0 = first_token([w for w, v in LOADS[a]], c)
-            tile = keep.tile([P, PACK, width], F32, name=f"raw{a}_{c}")
+        def load_tokens(a, c):
+            width, t0 = LOADS[a][c][0], first_token(a, c)
+            raw[a, c] = keep.tile([P, PACK, width], F32, name=f"raw{a}_{c}")
             rows = xT[a * K_PASS : (a + 1) * K_PASS, t0 : t0 + width]
-            nc.sync.dma_start(out=tile[:], in_=rows.rearrange("(p j) w -> p j w", j=PACK))
-            raw[a, c] = tile
+            nc.sync.dma_start(out=raw[a, c][:], in_=rows.rearrange("(p j) w -> p j w", j=PACK))
 
         for c in range(len(LOADS[0])):
-            load_chunk(0, c)
+            load_tokens(0, c)
         nc.sync.dma_start(offs_sb[:], offs)
         for c in range(len(LOADS[1])):
-            load_chunk(1, c)
+            load_tokens(1, c)
 
-        for planes, scales in ((w8_planes, w8_scales), (w4_planes, w4_scales)):
+        for scales_sb, scales in ((w8_scales_sb, w8_scales), (w4_scales_sb, w4_scales)):
             for q in range(4):
                 nc.sync.dma_start(
-                    out=planes[32 * q : 32 * q + 4, :].bitcast(I32).rearrange("q (e n) -> q e n", e=E),
-                    in_=scales[:, 0, 4 * q : 4 * q + 4, :].bitcast(I32).rearrange("e q n -> q e n"),
+                    out=scales_sb[32 * q : 32 * q + 4, :].bitcast(I32).rearrange("r (e n) -> r e n", e=E),
+                    in_=scales[:, 0, 4 * q : 4 * q + 4, :].bitcast(I32).rearrange("e r n -> r e n"),
                 )
         nc.sync.dma_start(bias[:], b)
         half = E // 2
@@ -111,12 +109,11 @@ def tile_moe_pln_lin_gelu_kernel(
 
         def interleave(a, c):
             width, by_vector = LOADS[a][c]
-            tile = keep.tile([P, width, PACK], BF16, name=f"grouped{a}_{c}", align_bytes=64)
-            grouped[a, c] = tile
+            grouped[a, c] = keep.tile([P, width, PACK], BF16, name=f"grouped{a}_{c}", align_bytes=64)
 
             def views(lo, hi):
-                dst = tile[:, lo:hi, :].rearrange("p (c i) t -> p c t i", i=2)
-                src = raw[a, c][:, :, lo:hi].rearrange("p t (c i) -> p c t i", i=2)
+                dst = grouped[a, c][:, lo:hi, :].rearrange("p (m i) j -> p m j i", i=2)
+                src = raw[a, c][:, :, lo:hi].rearrange("p j (m i) -> p m j i", i=2)
                 return dst, src
 
             if by_vector < width:
@@ -127,9 +124,9 @@ def tile_moe_pln_lin_gelu_kernel(
                 nc.vector.tensor_copy(dst, src)
 
         def quantise(a, c):
-            t0 = first_token([w for w, v in LOADS[a]], c)
-            for q, width in enumerate(QUANTS[a][c]):
-                lo = first_token(QUANTS[a][c], q)
+            t0 = first_token(a, c)
+            for call, width in enumerate(QUANTS[a][c]):
+                lo = sum(QUANTS[a][c][:call])
                 hi = lo + width
                 nc.vector.quantize_mx(
                     out=x_words[a][:, t0 + lo : t0 + hi].bitcast(FP8X4),
@@ -140,29 +137,29 @@ def tile_moe_pln_lin_gelu_kernel(
         def gather(dst, window, lo, hi):
             nc.vector.tensor_copy(dst[:, lo:hi], window[:].indirect(offs_sb[:, lo // 16 : hi // 16]))
 
-        for c in range(3):
+        for c in range(len(LOADS[0])):
             interleave(0, c)
             quantise(0, c)
-        for c in range(3):
+        final_load = len(LOADS[1]) - 1
+        for c in range(final_load):
             interleave(1, c)
-        gather(slot_words[0], x_words[0], 0, 1024)
-        gather(slot_words[0], x_words[0], 1024, 2048)
-        gather(slot_words[0], x_words[0], 2048, 3072)
-        quantise(1, 0)
-        quantise(1, 1)
-        interleave(1, 3)
-        quantise(1, 2)
-        quantise(1, 3)
+        for lo in range(0, S, THIRD):
+            gather(slot_words[0], x_words[0], lo, lo + THIRD)
+        for c in range(final_load - 1):
+            quantise(1, c)
+        interleave(1, final_load)
+        quantise(1, final_load - 1)
+        quantise(1, final_load)
 
-        banks = {}
+        sums = {}
+        expert_bank = {}
 
         def first_pass(e, g):
-            bank = banks[e, g]
             cols = slice(e * C + g * GROUP, e * C + (g + 1) * GROUP)
             nc.tensor.matmul_mx(
-                out=bank,
+                out=sums[e, g],
                 lhsT=w8_sb[:, e * N * 4 : (e + 1) * N * 4].bitcast(FP8X4),
-                lhsT_scale=w8_planes[:, e * N : (e + 1) * N],
+                lhsT_scale=w8_scales_sb[:, e * N : (e + 1) * N],
                 rhs=slot_words[0][:, cols].bitcast(FP8X4),
                 rhs_scale=slot_scales[SCALE_ROW[0] : P, cols],
                 start=True,
@@ -170,117 +167,115 @@ def tile_moe_pln_lin_gelu_kernel(
             )
 
         def second_pass(e, g):
-            bank = banks[e, g]
             cols = slice(e * C + g * GROUP, e * C + (g + 1) * GROUP)
             nc.tensor.matmul_mx(
-                out=bank,
+                out=sums[e, g],
                 lhsT=w4_sb[:, e * N * 2 : (e + 1) * N * 2].bitcast(FP4X4),
-                lhsT_scale=w4_planes[:, e * N : (e + 1) * N],
+                lhsT_scale=w4_scales_sb[:, e * N : (e + 1) * N],
                 rhs=slot_words[1][:, cols].bitcast(FP8X4),
                 rhs_scale=slot_scales[SCALE_ROW[1] : P, cols],
                 start=False,
                 stop=True,
             )
 
-        def gelu(e, bank, lo, hi):
-            nc.scalar.activation(y[:, lo:hi], bank, ACT.Gelu_apprx_tanh, bias=bias[:, e : e + 1])
+        def gelu(e, source, lo, hi):
+            nc.scalar.activation(y[:, lo:hi], source, ACT.Gelu_apprx_tanh, bias=bias[:, e : e + 1])
 
         last = E - 1
-        tail_banks = [psum.tile([P, GROUP], F32, name=f"tail{g}") for g in range(2)]
+        last_banks = [psum.tile([P, GROUP], F32, name=f"last{g}") for g in range(2)]
         for g in range(2):
-            banks[last, g] = tail_banks[g][:]
+            sums[last, g] = last_banks[g][:]
 
         def open_bank(e):
-            bank = psum.tile([P, C], F32, name=f"bank{e % 6}")
-            banks[e] = bank
+            expert_bank[e] = psum.tile([P, C], F32, name=f"bank{e % EXPERT_BANKS}")
             for g in range(2):
-                banks[e, g] = bank[:, g * GROUP : (g + 1) * GROUP]
+                sums[e, g] = expert_bank[e][:, g * GROUP : (g + 1) * GROUP]
             first_pass(e, 0)
 
-        def expert(e):
-            if e not in banks:
-                open_bank(e)
+        def finish_expert(e):
             second_pass(e, 0)
             first_pass(e, 1)
             second_pass(e, 1)
-            gelu(e, banks[e][:], e * C, (e + 1) * C)
+            gelu(e, expert_bank[e][:], e * C, (e + 1) * C)
 
-        for lo in range(0, S, 1024):
-            gather(slot_scales, x_scales, lo, lo + 1024)
-            if lo == 2048:
-                for e in range(lo // C, last):
-                    open_bank(e)
-                for g in range(2):
-                    first_pass(last, g)
-                cuts = (2048, 2304, 2560, 2816)
-            else:
-                cuts = (lo, lo + 1024)
-            for a0, a1 in zip(cuts[:-1], cuts[1:]):
-                gather(slot_words[1], x_words[1], a0, a1)
-                for e in range(a0 // C, a1 // C):
-                    expert(e)
-        gather(slot_words[1], x_words[1], 2816, 3072)
+        last_third = S - THIRD
+        for lo in range(0, last_third, THIRD):
+            gather(slot_scales, x_scales, lo, lo + THIRD)
+            gather(slot_words[1], x_words[1], lo, lo + THIRD)
+            for e in range(lo // C, (lo + THIRD) // C):
+                open_bank(e)
+                finish_expert(e)
+        gather(slot_scales, x_scales, last_third, S)
+        for e in range(last_third // C, last):
+            open_bank(e)
+        for g in range(2):
+            first_pass(last, g)
+        for e in range(last_third // C, last):
+            gather(slot_words[1], x_words[1], e * C, (e + 1) * C)
+            finish_expert(e)
+        gather(slot_words[1], x_words[1], last * C, S)
         for g in range(2):
             second_pass(last, g)
-            gelu(last, banks[last, g], last * C + g * GROUP, last * C + (g + 1) * GROUP)
+            gelu(last, sums[last, g], last * C + g * GROUP, last * C + (g + 1) * GROUP)
 
-        pieces = ((0, 384), (384, 640), (640, 896), (896, 1152), (1152, 1408), (1408, 1536))
         picked = {}
+        turned = {}
 
-        def pick(r, i):
-            lo, hi = pieces[i]
+        def pick(r, piece):
+            lo, hi = piece
             pos = (pos1_sb, pos2_sb)[r]
-            tile = keep.tile([P, hi - lo], F32, name=f"picked{r}_{i}")
-            nc.vector.tensor_tensor(tile[:], y[:].indirect(pos[:, lo // 16 : hi // 16]), gates[:, r, lo:hi], MULT)
-            picked[r, i] = tile
+            picked[r, piece] = keep.tile([P, hi - lo], F32, name=f"picked{r}_{lo}")
+            nc.vector.tensor_tensor(
+                picked[r, piece][:], y[:].indirect(pos[:, lo // 16 : hi // 16]), gates[:, r, lo:hi], MULT
+            )
 
-        def combine(i):
-            lo, hi = pieces[i]
-            total = keep.tile([P, hi - lo], F32, name=f"total{i}")
-            nc.vector.tensor_tensor(total[:], picked[0, i][:], picked[1, i][:], ADD)
+        def add_on_vector(piece):
+            lo, hi = piece
+            total = keep.tile([P, hi - lo], F32, name=f"total{lo}")
+            nc.vector.tensor_tensor(total[:], picked[0, piece][:], picked[1, piece][:], ADD)
             nc.sync.dma_start(out[:, lo:hi], total[:])
 
-        turned_sb = {}
+        def blocks(piece):
+            return [slice(c, c + P) for c in range(0, piece[1] - piece[0], P)]
 
-        def blocks(i):
-            lo, hi = pieces[i]
-            return [slice(c, c + P) for c in range(0, hi - lo, P)]
-
-        def turn_and_add(i):
-            lo, hi = pieces[i]
-            turned = psum.tile([P, hi - lo], F32, name=f"bank{i % 2}")
-            for block in blocks(i):
+        def add_turned(i):
+            piece = TENSOR_PIECES[i]
+            width = piece[1] - piece[0]
+            bank = psum.tile([P, width], F32, name=f"bank{i % 2}")
+            for block in blocks(piece):
                 for r in range(2):
                     nc.tensor.matmul(
-                        turned[:, block],
-                        lhsT=picked[r, i][:, block],
+                        bank[:, block],
+                        lhsT=picked[r, piece][:, block],
                         rhs=identity[:],
                         start=(r == 0),
                         stop=(r == 1),
                         is_transpose=True,
                     )
-            turned_sb[i] = keep.tile([P, hi - lo], F32, name=f"turned{i}")
-            nc.scalar.copy(turned_sb[i][:], turned[:])
+            turned[i] = keep.tile([P, width], F32, name=f"turned{i}")
+            nc.scalar.copy(turned[i][:], bank[:])
 
         def turn_back(i):
-            lo, hi = pieces[i]
-            back = psum.tile([P, hi - lo], F32, name=f"bank{2 + i}")
-            for block in blocks(i):
-                nc.tensor.transpose(back[:, block], turned_sb[i][:, block], identity[:])
-            total = keep.tile([P, hi - lo], F32, name=f"total{i}")
-            nc.scalar.copy(total[:], back[:])
+            piece = TENSOR_PIECES[i]
+            lo, hi = piece
+            bank = psum.tile([P, hi - lo], F32, name=f"bank{2 + i}")
+            for block in blocks(piece):
+                nc.tensor.transpose(bank[:, block], turned[i][:, block], identity[:])
+            total = keep.tile([P, hi - lo], F32, name=f"total{lo}")
+            nc.scalar.copy(total[:], bank[:])
             nc.scalar.dma_start(out[:, lo:hi], total[:])
 
-        for i in range(4):
-            pick(0, i)
-            pick(1, i)
-            turn_and_add(i)
+        for i, piece in enumerate(TENSOR_PIECES):
+            pick(0, piece)
+            pick(1, piece)
+            add_turned(i)
             if i > 0:
                 turn_back(i - 1)
-        turn_back(3)
-        pick(0, 4)
-        pick(1, 4)
-        pick(0, 5)
-        combine(4)
-        pick(1, 5)
-        combine(5)
+        turn_back(len(TENSOR_PIECES) - 1)
+        before_last, very_last = VECTOR_PIECES
+        pick(0, before_last)
+        pick(1, before_last)
+        pick(0, very_last)
+        add_on_vector(before_last)
+        pick(1, very_last)
+        add_on_vector(very_last)

@@ -31,7 +31,7 @@ LOADS = (
 )
 QUANTS = (((512, 256), (256, 256), (256,)), ((256,), (256, 128), (512,), (256, 128)))
 SCALE_ROW = (4, 0)
-TENSOR_PIECES = ((0, 384), (384, 640), (640, 896), (896, 1152))
+TENSOR_PIECES = ((0, 384), (384, 768), (768, 1024), (1024, 1152))
 VECTOR_PIECES = ((1152, 1408), (1408, 1536))
 
 
@@ -229,10 +229,11 @@ def tile_moe_pln_lin_gelu_kernel(
                 picked[r, piece][:], y[:].indirect(pos[:, lo // 16 : hi // 16]), gates[:, r, lo:hi], MULT
             )
 
-        def add_on_vector(piece):
+        def add_on_vector(piece, both):
             lo, hi = piece
             total = keep.tile([P, hi - lo], F32, name=f"total{lo}")
-            nc.vector.tensor_tensor(total[:], picked[0, piece][:], picked[1, piece][:], ADD)
+            first = picked[0, both][:, lo - both[0] : hi - both[0]]
+            nc.vector.tensor_tensor(total[:], first, picked[1, piece][:], ADD)
             nc.sync.dma_start(out[:, lo:hi], total[:])
 
         def blocks(piece):
@@ -242,14 +243,14 @@ def tile_moe_pln_lin_gelu_kernel(
             piece = TENSOR_PIECES[i]
             width = piece[1] - piece[0]
             bank = psum.tile([P, width], F32, name=f"bank{i % 2}")
-            for block in blocks(piece):
-                for r in range(2):
+            for r in range(2):
+                for block in blocks(piece):
                     nc.tensor.matmul(
                         bank[:, block],
                         lhsT=picked[r, piece][:, block],
                         rhs=identity[:],
-                        start=(r == 0),
-                        stop=(r == 1),
+                        start=(r == 0 and block.start == 0),
+                        stop=(r == 1 and block.stop == width),
                         is_transpose=True,
                     )
             turned[i] = keep.tile([P, width], F32, name=f"turned{i}")
@@ -272,10 +273,9 @@ def tile_moe_pln_lin_gelu_kernel(
             if i > 0:
                 turn_back(i - 1)
         turn_back(len(TENSOR_PIECES) - 1)
-        before_last, very_last = VECTOR_PIECES
-        pick(0, before_last)
-        pick(1, before_last)
-        pick(0, very_last)
-        add_on_vector(before_last)
-        pick(1, very_last)
-        add_on_vector(very_last)
+        both = (VECTOR_PIECES[0][0], VECTOR_PIECES[-1][1])
+        pick(0, both)
+        for piece in VECTOR_PIECES:
+            pick(1, piece)
+        for piece in VECTOR_PIECES:
+            add_on_vector(piece, both)

@@ -11,8 +11,8 @@ P = 128
 PACK = 4
 K_PASS = P * PACK
 GROUP = 128
-THIRD = S // 3
-EXPERT_BANKS = 6
+HALF = S // 2
+WINDOW = 2048
 
 F32 = mybir.dt.float32
 BF16 = mybir.dt.bfloat16
@@ -27,10 +27,16 @@ MULT, ADD = mybir.AluOpType.mult, mybir.AluOpType.add
 
 LOADS = (
     ((768, 512), (512, 256), (256, 160)),
-    ((256, 0), (384, 0), (512, 0), (384, 128)),
+    ((512, 0), (448, 0), (320, 0), (256, 0)),
 )
-QUANTS = (((512, 256), (256, 256), (256,)), ((256,), (256, 128), (512,), (256, 128)))
+QUANTS = (((512, 256), (256, 256), (256,)), (1024, 256, 256))
 SCALE_ROW = (4, 0)
+RUNS = ((6,), (2, 2, 1, 1))
+BANK_SLOTS = tuple((lo, lo + 2 * C) for lo in range(0, 10 * C, 2 * C)) + (
+    (10 * C, 11 * C),
+    (11 * C, 11 * C + GROUP),
+    (11 * C + GROUP, 12 * C),
+)
 TENSOR_PIECES = ((0, 384), (384, 768), (768, 1024), (1024, 1152))
 VECTOR_PIECES = ((1152, 1408), (1408, 1536))
 
@@ -48,8 +54,8 @@ def tile_moe_pln_lin_gelu_kernel(
         pos1_sb = lists.tile([P, T // 16], U16, name="pos1_sb")
         pos2_sb = lists.tile([P, T // 16], U16, name="pos2_sb")
 
-        x_words = [keep.tile([P, T], U32, name=f"x_words{a}", align_bytes=64) for a in range(2)]
-        x_scales = keep.tile([P, T], U8, name="x_scales", align_bytes=64)
+        x_words = [keep.tile([P, WINDOW], U32, name=f"x_words{a}", align_bytes=64) for a in range(2)]
+        x_scales = keep.tile([P, WINDOW], U8, name="x_scales", align_bytes=64)
         slot_words = [keep.tile([P, S], U32, name=f"slot_words{a}", align_bytes=64) for a in range(2)]
         slot_scales = keep.tile([P, S], U8, name="slot_scales", align_bytes=64)
         w8_sb = keep.tile([P, E * N * 4], U8, name="w8_sb", align_bytes=64)
@@ -63,6 +69,8 @@ def tile_moe_pln_lin_gelu_kernel(
 
         nc.gpsimd.memset(x_scales[:], 0)
         make_identity(nc, identity[:])
+        for a in range(2):
+            nc.vector.memset(x_words[a][:, T:].bitcast(I32), 0)
         nc.vector.memset(w8_scales_sb[:].bitcast(I32), 0)
         nc.vector.memset(w4_scales_sb[:].bitcast(I32), 0)
 
@@ -106,10 +114,14 @@ def tile_moe_pln_lin_gelu_kernel(
         nc.sync.dma_start(gates[:], gate.rearrange("r p t -> p r t"))
 
         grouped = {}
+        grouped_second = keep.tile([P, T, PACK], BF16, name="grouped_second", align_bytes=64)
 
         def interleave(a, c):
             width, by_vector = LOADS[a][c]
-            grouped[a, c] = keep.tile([P, width, PACK], BF16, name=f"grouped{a}_{c}", align_bytes=64)
+            if a == 0:
+                grouped[a, c] = keep.tile([P, width, PACK], BF16, name=f"grouped{a}_{c}", align_bytes=64)[:]
+            else:
+                grouped[a, c] = grouped_second[:, first_token(a, c) : first_token(a, c) + width, :]
 
             def views(lo, hi):
                 dst = grouped[a, c][:, lo:hi, :].rearrange("p (m i) j -> p m j i", i=2)
@@ -123,15 +135,14 @@ def tile_moe_pln_lin_gelu_kernel(
                 dst, src = views(0, by_vector)
                 nc.vector.tensor_copy(dst, src)
 
-        def quantise(a, c):
-            t0 = first_token(a, c)
-            for call, width in enumerate(QUANTS[a][c]):
-                lo = sum(QUANTS[a][c][:call])
+        def quantise(a, source, t0, widths):
+            for call, width in enumerate(widths):
+                lo = sum(widths[:call])
                 hi = lo + width
                 nc.vector.quantize_mx(
                     out=x_words[a][:, t0 + lo : t0 + hi].bitcast(FP8X4),
                     scales=x_scales[SCALE_ROW[a] : P, t0 + lo : t0 + hi],
-                    in_=grouped[a, c][:, lo:hi, :].rearrange("p w j -> p (w j)"),
+                    in_=source[:, lo:hi, :].rearrange("p w j -> p (w j)"),
                 )
 
         def gather(dst, window, lo, hi):
@@ -139,84 +150,73 @@ def tile_moe_pln_lin_gelu_kernel(
 
         for c in range(len(LOADS[0])):
             interleave(0, c)
-            quantise(0, c)
-        final_load = len(LOADS[1]) - 1
-        for c in range(final_load):
+            quantise(0, grouped[0, c], first_token(0, c), QUANTS[0][c])
+        for c in range(len(LOADS[1])):
             interleave(1, c)
-        for lo in range(0, S, THIRD):
-            gather(slot_words[0], x_words[0], lo, lo + THIRD)
-        for c in range(final_load - 1):
-            quantise(1, c)
-        interleave(1, final_load)
-        quantise(1, final_load - 1)
-        quantise(1, final_load)
+        for lo in range(0, S, HALF):
+            gather(slot_words[0], x_words[0], lo, lo + HALF)
+        quantise(1, grouped_second, 0, QUANTS[1])
 
-        sums = {}
-        expert_bank = {}
-
-        def first_pass(e, g):
-            cols = slice(e * C + g * GROUP, e * C + (g + 1) * GROUP)
+        def first_pass(target, lo, hi, start):
+            e = lo // C
             nc.tensor.matmul_mx(
-                out=sums[e, g],
+                out=target,
                 lhsT=w8_sb[:, e * N * 4 : (e + 1) * N * 4].bitcast(FP8X4),
                 lhsT_scale=w8_scales_sb[:, e * N : (e + 1) * N],
-                rhs=slot_words[0][:, cols].bitcast(FP8X4),
-                rhs_scale=slot_scales[SCALE_ROW[0] : P, cols],
-                start=True,
+                rhs=slot_words[0][:, lo:hi].bitcast(FP8X4),
+                rhs_scale=slot_scales[SCALE_ROW[0] : P, lo:hi],
+                start=start,
                 stop=False,
             )
 
-        def second_pass(e, g):
-            cols = slice(e * C + g * GROUP, e * C + (g + 1) * GROUP)
+        def second_pass(target, lo, hi, stop):
+            e = lo // C
             nc.tensor.matmul_mx(
-                out=sums[e, g],
+                out=target,
                 lhsT=w4_sb[:, e * N * 2 : (e + 1) * N * 2].bitcast(FP4X4),
                 lhsT_scale=w4_scales_sb[:, e * N : (e + 1) * N],
-                rhs=slot_words[1][:, cols].bitcast(FP8X4),
-                rhs_scale=slot_scales[SCALE_ROW[1] : P, cols],
+                rhs=slot_words[1][:, lo:hi].bitcast(FP8X4),
+                rhs_scale=slot_scales[SCALE_ROW[1] : P, lo:hi],
                 start=False,
-                stop=True,
+                stop=stop,
             )
 
-        def gelu(e, source, lo, hi):
-            nc.scalar.activation(y[:, lo:hi], source, ACT.Gelu_apprx_tanh, bias=bias[:, e : e + 1])
+        banks = {}
 
-        last = E - 1
-        last_banks = [psum.tile([P, GROUP], F32, name=f"last{g}") for g in range(2)]
-        for g in range(2):
-            sums[last, g] = last_banks[g][:]
+        def open_bank(index):
+            lo, hi = BANK_SLOTS[index]
+            banks[index] = psum.tile([P, hi - lo], F32, name=f"bank{index}")
+            step = min(C, hi - lo)
+            for s0 in range(lo, hi, step):
+                first_pass(banks[index][:, s0 - lo : s0 - lo + step], s0, s0 + step, s0 == lo)
 
-        def open_bank(e):
-            expert_bank[e] = psum.tile([P, C], F32, name=f"bank{e % EXPERT_BANKS}")
-            for g in range(2):
-                sums[e, g] = expert_bank[e][:, g * GROUP : (g + 1) * GROUP]
-            first_pass(e, 0)
+        def close_bank(index):
+            lo, hi = BANK_SLOTS[index]
+            for s0 in range(lo, hi, GROUP):
+                second_pass(banks[index][:, s0 - lo : s0 - lo + GROUP], s0, s0 + GROUP, s0 + GROUP == hi)
+            step = min(C, hi - lo)
+            for s0 in range(lo, hi, step):
+                e = s0 // C
+                nc.scalar.activation(
+                    y[:, s0 : s0 + step],
+                    banks[index][:, s0 - lo : s0 - lo + step],
+                    ACT.Gelu_apprx_tanh,
+                    bias=bias[:, e : e + 1],
+                )
 
-        def finish_expert(e):
-            second_pass(e, 0)
-            first_pass(e, 1)
-            second_pass(e, 1)
-            gelu(e, expert_bank[e][:], e * C, (e + 1) * C)
+        def banks_within(lo, hi):
+            return [index for index, (first, end) in enumerate(BANK_SLOTS) if lo <= first and end <= hi]
 
-        last_third = S - THIRD
-        for lo in range(0, last_third, THIRD):
-            gather(slot_scales, x_scales, lo, lo + THIRD)
-            gather(slot_words[1], x_words[1], lo, lo + THIRD)
-            for e in range(lo // C, (lo + THIRD) // C):
-                open_bank(e)
-                finish_expert(e)
-        gather(slot_scales, x_scales, last_third, S)
-        for e in range(last_third // C, last):
-            open_bank(e)
-        for g in range(2):
-            first_pass(last, g)
-        for e in range(last_third // C, last):
-            gather(slot_words[1], x_words[1], e * C, (e + 1) * C)
-            finish_expert(e)
-        gather(slot_words[1], x_words[1], last * C, S)
-        for g in range(2):
-            second_pass(last, g)
-            gelu(last, sums[last, g], last * C + g * GROUP, last * C + (g + 1) * GROUP)
+        for h, runs in enumerate(RUNS):
+            lo = h * HALF
+            gather(slot_scales, x_scales, lo, lo + HALF)
+            for index in banks_within(lo, lo + HALF):
+                open_bank(index)
+            for run in runs:
+                gather(slot_words[1], x_words[1], lo, lo + run * C)
+                for index in banks_within(lo, lo + run * C):
+                    close_bank(index)
+                lo = lo + run * C
 
         picked = {}
         turned = {}

@@ -31,14 +31,14 @@ LOADS = (
 )
 QUANTS = (((512, 256), (256, 256), (256,)), (1024, 256, 256))
 SCALE_ROW = (4, 0)
-RUNS = ((6,), (2, 2, 1, 1))
+RUNS = ((8,), (2, 1, 1))
 BANK_SLOTS = tuple((lo, lo + 2 * C) for lo in range(0, 10 * C, 2 * C)) + (
     (10 * C, 11 * C),
     (11 * C, 11 * C + GROUP),
     (11 * C + GROUP, 12 * C),
 )
 TENSOR_PIECES = ((0, 384), (384, 768), (768, 1024), (1024, 1152))
-VECTOR_PIECES = ((1152, 1408), (1408, 1536))
+VECTOR_PIECES = ((1152, 1344), (1344, 1536))
 
 
 def tile_moe_pln_lin_gelu_kernel(
@@ -54,8 +54,8 @@ def tile_moe_pln_lin_gelu_kernel(
         pos1_sb = lists.tile([P, T // 16], U16, name="pos1_sb")
         pos2_sb = lists.tile([P, T // 16], U16, name="pos2_sb")
 
-        x_words = [keep.tile([P, WINDOW], U32, name=f"x_words{a}", align_bytes=64) for a in range(2)]
-        x_scales = keep.tile([P, WINDOW], U8, name="x_scales", align_bytes=64)
+        x_words = [keep.tile([P, (a + 1) * WINDOW], U32, name=f"x_words{a}", align_bytes=64) for a in range(2)]
+        x_scales = keep.tile([P, 2 * WINDOW], U8, name="x_scales", align_bytes=64)
         slot_words = [keep.tile([P, S], U32, name=f"slot_words{a}", align_bytes=64) for a in range(2)]
         slot_scales = keep.tile([P, S], U8, name="slot_scales", align_bytes=64)
         w8_sb = keep.tile([P, E * N * 4], U8, name="w8_sb", align_bytes=64)
@@ -67,10 +67,10 @@ def tile_moe_pln_lin_gelu_kernel(
         y = keep.tile([P, S], F32, name="y")
         identity = keep.tile([P, P], F32, name="identity")
 
-        nc.gpsimd.memset(x_scales[:], 0)
+        nc.vector.memset(x_scales[:].bitcast(I32), 0)
         make_identity(nc, identity[:])
         for a in range(2):
-            nc.vector.memset(x_words[a][:, T:].bitcast(I32), 0)
+            nc.vector.memset(x_words[a][:, T : (a + 1) * WINDOW].bitcast(I32), 0)
         nc.vector.memset(w8_scales_sb[:].bitcast(I32), 0)
         nc.vector.memset(w4_scales_sb[:].bitcast(I32), 0)
 
@@ -146,7 +146,8 @@ def tile_moe_pln_lin_gelu_kernel(
                 )
 
         def gather(dst, window, lo, hi):
-            nc.vector.tensor_copy(dst[:, lo:hi], window[:].indirect(offs_sb[:, lo // 16 : hi // 16]))
+            columns = 2 * WINDOW if hi - lo > HALF else WINDOW
+            nc.vector.tensor_copy(dst[:, lo:hi], window[:, :columns].indirect(offs_sb[:, lo // 16 : hi // 16]))
 
         for c in range(len(LOADS[0])):
             interleave(0, c)
@@ -207,10 +208,11 @@ def tile_moe_pln_lin_gelu_kernel(
         def banks_within(lo, hi):
             return [index for index, (first, end) in enumerate(BANK_SLOTS) if lo <= first and end <= hi]
 
-        for h, runs in enumerate(RUNS):
-            lo = h * HALF
-            gather(slot_scales, x_scales, lo, lo + HALF)
-            for index in banks_within(lo, lo + HALF):
+        lo = 0
+        for runs in RUNS:
+            end = lo + sum(runs) * C
+            gather(slot_scales, x_scales, lo, end)
+            for index in banks_within(lo, end):
                 open_bank(index)
             for run in runs:
                 gather(slot_words[1], x_words[1], lo, lo + run * C)

@@ -37,8 +37,10 @@ BANK_SLOTS = tuple((lo, lo + 2 * C) for lo in range(0, 10 * C, 2 * C)) + (
     (11 * C, 11 * C + GROUP),
     (11 * C + GROUP, 12 * C),
 )
-TENSOR_PIECES = ((0, 384), (384, 768), (768, 1024), (1024, 1152))
-VECTOR_PIECES = ((1152, 1344), (1344, 1536))
+SHARED_PIECES = ((0, 256), (256, 640), (640, 1024), (1024, 1280))
+SHARED_END = SHARED_PIECES[-1][1]
+FIRST_PICKS = ((0, 640), (640, 1280), (1280, 1536))
+VECTOR_ADDS = ((1280, 1536),)
 
 
 def tile_moe_pln_lin_gelu_kernel(
@@ -48,6 +50,7 @@ def tile_moe_pln_lin_gelu_kernel(
     with ExitStack() as ctx:
         lists = ctx.enter_context(tc.tile_pool(name="lists", bufs=1))
         keep = ctx.enter_context(tc.tile_pool(name="keep", bufs=1))
+        small = ctx.enter_context(tc.tile_pool(name="small", bufs=1))
         psum = ctx.enter_context(tc.psum_pool(name="psum", bufs=1))
 
         offs_sb = lists.tile([P, S // 16], U16, name="offs_sb")
@@ -63,7 +66,8 @@ def tile_moe_pln_lin_gelu_kernel(
         w8_scales_sb = keep.tile([P, E * N], U8, name="w8_scales_sb", align_bytes=64)
         w4_scales_sb = keep.tile([P, E * N], U8, name="w4_scales_sb", align_bytes=64)
         bias = keep.tile([P, E], F32, name="bias")
-        gates = keep.tile([P, 2, T], F32, name="gates")
+        gate0 = keep.tile([P, T], F32, name="gate0")
+        gate1 = keep.tile([P, T - SHARED_END], F32, name="gate1")
         y = keep.tile([P, S], F32, name="y")
         identity = keep.tile([P, P], F32, name="identity")
 
@@ -111,7 +115,8 @@ def tile_moe_pln_lin_gelu_kernel(
             )
         nc.sync.dma_start(pos1_sb[:], pos1)
         nc.sync.dma_start(pos2_sb[:], pos2)
-        nc.sync.dma_start(gates[:], gate.rearrange("r p t -> p r t"))
+        nc.sync.dma_start(gate0[:], gate[0])
+        nc.sync.dma_start(gate1[:], gate[1, :, SHARED_END:T])
 
         grouped = {}
         grouped_second = keep.tile([P, T, PACK], BF16, name="grouped_second", align_bytes=64)
@@ -157,6 +162,10 @@ def tile_moe_pln_lin_gelu_kernel(
         for lo in range(0, S, HALF):
             gather(slot_words[0], x_words[0], lo, lo + HALF)
         quantise(1, grouped_second, 0, QUANTS[1])
+
+        gate1_columns = small.tile([P, SHARED_END // P], F32, name="gate1_columns")
+        with nc.allow_non_contiguous_dma(reason="one value a partition"):
+            nc.sync.dma_start(gate1_columns[:], gate[1, 0, 0:SHARED_END].rearrange("(c p) -> p c", p=P))
 
         def first_pass(target, lo, hi, start):
             e = lo // C
@@ -220,64 +229,55 @@ def tile_moe_pln_lin_gelu_kernel(
                     close_bank(index)
                 lo = lo + run * C
 
-        picked = {}
-        turned = {}
-
-        def pick(r, piece):
-            lo, hi = piece
-            pos = (pos1_sb, pos2_sb)[r]
-            picked[r, piece] = keep.tile([P, hi - lo], F32, name=f"picked{r}_{lo}")
-            nc.vector.tensor_tensor(
-                picked[r, piece][:], y[:].indirect(pos[:, lo // 16 : hi // 16]), gates[:, r, lo:hi], MULT
-            )
-
-        def add_on_vector(piece, both):
-            lo, hi = piece
-            total = keep.tile([P, hi - lo], F32, name=f"total{lo}")
-            first = picked[0, both][:, lo - both[0] : hi - both[0]]
-            nc.vector.tensor_tensor(total[:], first, picked[1, piece][:], ADD)
-            nc.sync.dma_start(out[:, lo:hi], total[:])
+        first = keep.tile([P, T], F32, name="first")
+        second_rest = keep.tile([P, T - SHARED_END], F32, name="second_rest")
+        scaled = {}
+        sums = {}
 
         def blocks(piece):
             return [slice(c, c + P) for c in range(0, piece[1] - piece[0], P)]
 
-        def add_turned(i):
-            piece = TENSOR_PIECES[i]
-            width = piece[1] - piece[0]
-            bank = psum.tile([P, width], F32, name=f"bank{i % 2}")
-            for r in range(2):
-                for block in blocks(piece):
-                    nc.tensor.matmul(
-                        bank[:, block],
-                        lhsT=picked[r, piece][:, block],
-                        rhs=identity[:],
-                        start=(r == 0 and block.start == 0),
-                        stop=(r == 1 and block.stop == width),
-                        is_transpose=True,
-                    )
-            turned[i] = keep.tile([P, width], F32, name=f"turned{i}")
-            nc.scalar.copy(turned[i][:], bank[:])
-
-        def turn_back(i):
-            piece = TENSOR_PIECES[i]
+        def pick_first(piece):
             lo, hi = piece
-            bank = psum.tile([P, hi - lo], F32, name=f"bank{2 + i}")
-            for block in blocks(piece):
-                nc.tensor.transpose(bank[:, block], turned[i][:, block], identity[:])
-            total = keep.tile([P, hi - lo], F32, name=f"total{lo}")
-            nc.scalar.copy(total[:], bank[:])
-            nc.scalar.dma_start(out[:, lo:hi], total[:])
+            nc.vector.tensor_tensor(first[:, lo:hi], y[:].indirect(pos1_sb[:, lo // 16 : hi // 16]), gate0[:, lo:hi], MULT)
 
-        for i, piece in enumerate(TENSOR_PIECES):
-            pick(0, piece)
-            pick(1, piece)
-            add_turned(i)
-            if i > 0:
-                turn_back(i - 1)
-        turn_back(len(TENSOR_PIECES) - 1)
-        both = (VECTOR_PIECES[0][0], VECTOR_PIECES[-1][1])
-        pick(0, both)
-        for piece in VECTOR_PIECES:
-            pick(1, piece)
-        for piece in VECTOR_PIECES:
-            add_on_vector(piece, both)
+        def pick_second(i):
+            lo, hi = SHARED_PIECES[i]
+            second = keep.tile([P, hi - lo], F32, name=f"second{i}", tag="second", bufs=2)
+            nc.scalar.activation(second[:], y[:].indirect(pos2_sb[:, lo // 16 : hi // 16]), ACT.Copy)
+            sums[i] = psum.tile([P, hi - lo], F32, name=f"bank{i % 2}")
+            for block in blocks(SHARED_PIECES[i]):
+                nc.tensor.transpose(sums[i][:, block], second[:, block], identity[:])
+
+        def scale_second(i):
+            lo, hi = SHARED_PIECES[i]
+            scaled[i] = keep.tile([P, hi - lo], F32, name=f"scaled{i}")
+            for block in blocks(SHARED_PIECES[i]):
+                column = (lo + block.start) // P
+                nc.scalar.activation(scaled[i][:, block], sums[i][:, block], ACT.Copy, scale=gate1_columns[:, column : column + 1])
+            sums[i] = psum.tile([P, hi - lo], F32, name=f"bank{2 + i}")
+            for block in blocks(SHARED_PIECES[i]):
+                nc.tensor.transpose(sums[i][:, block], scaled[i][:, block], identity[:])
+
+        def add_and_store(piece, second):
+            lo, hi = piece
+            total = keep.tile([P, hi - lo], F32, name=f"total{lo}")
+            nc.vector.tensor_tensor(total[:], second, first[:, lo:hi], ADD)
+            nc.sync.dma_start(out[:, lo:hi], total[:])
+
+        last = len(SHARED_PIECES) - 1
+        pick_first(FIRST_PICKS[0])
+        pick_first(FIRST_PICKS[1])
+        pick_second(0)
+        for i in range(last):
+            pick_second(i + 1)
+            scale_second(i)
+        scale_second(last)
+        add_and_store(SHARED_PIECES[0], sums[0][:])
+        pick_first(FIRST_PICKS[2])
+        add_and_store(SHARED_PIECES[1], sums[1][:])
+        nc.vector.tensor_tensor(second_rest[:], y[:].indirect(pos2_sb[:, SHARED_END // 16 : T // 16]), gate1[:], MULT)
+        for i in range(2, last + 1):
+            add_and_store(SHARED_PIECES[i], sums[i][:])
+        for lo, hi in VECTOR_ADDS:
+            add_and_store((lo, hi), second_rest[:, lo - SHARED_END : hi - SHARED_END])

@@ -37,10 +37,10 @@ BANK_SLOTS = tuple((lo, lo + 2 * C) for lo in range(0, 10 * C, 2 * C)) + (
     (11 * C, 11 * C + GROUP),
     (11 * C + GROUP, 12 * C),
 )
-SHARED_PIECES = ((0, 256), (256, 640), (640, 1024), (1024, 1280))
-SHARED_END = SHARED_PIECES[-1][1]
-FIRST_PICKS = ((0, 640), (640, 1280), (1280, 1536))
-VECTOR_ADDS = ((1280, 1536),)
+SHARED_START = 256
+FIRST_PICKS = ((0, 512), (512, 1024), (1024, 1536))
+SECOND_PICKS = ((256, 768), (768, 1280), (1280, 1536))
+SHARED_ADDS = ((256, 640), (640, 1024), (1024, 1280), (1280, 1536))
 
 
 def tile_moe_pln_lin_gelu_kernel(
@@ -67,7 +67,7 @@ def tile_moe_pln_lin_gelu_kernel(
         w4_scales_sb = keep.tile([P, E * N], U8, name="w4_scales_sb", align_bytes=64)
         bias = keep.tile([P, E], F32, name="bias")
         gate0 = keep.tile([P, T], F32, name="gate0")
-        gate1 = keep.tile([P, T - SHARED_END], F32, name="gate1")
+        gate1 = keep.tile([P, SHARED_START], F32, name="gate1")
         y = keep.tile([P, S], F32, name="y")
         identity = keep.tile([P, P], F32, name="identity")
 
@@ -116,7 +116,7 @@ def tile_moe_pln_lin_gelu_kernel(
         nc.sync.dma_start(pos1_sb[:], pos1)
         nc.sync.dma_start(pos2_sb[:], pos2)
         nc.sync.dma_start(gate0[:], gate[0])
-        nc.sync.dma_start(gate1[:], gate[1, :, SHARED_END:T])
+        nc.sync.dma_start(gate1[:], gate[1, :, 0:SHARED_START])
 
         grouped = {}
         grouped_second = keep.tile([P, T, PACK], BF16, name="grouped_second", align_bytes=64)
@@ -163,9 +163,9 @@ def tile_moe_pln_lin_gelu_kernel(
             gather(slot_words[0], x_words[0], lo, lo + HALF)
         quantise(1, grouped_second, 0, QUANTS[1])
 
-        gate1_columns = small.tile([P, SHARED_END // P], F32, name="gate1_columns")
+        gate1_columns = small.tile([P, (T - SHARED_START) // P], F32, name="gate1_columns")
         with nc.allow_non_contiguous_dma(reason="one value a partition"):
-            nc.sync.dma_start(gate1_columns[:], gate[1, 0, 0:SHARED_END].rearrange("(c p) -> p c", p=P))
+            nc.sync.dma_start(gate1_columns[:], gate[1, 0, SHARED_START:T].rearrange("(c p) -> p c", p=P))
 
         def first_pass(target, lo, hi, start):
             e = lo // C
@@ -230,54 +230,39 @@ def tile_moe_pln_lin_gelu_kernel(
                 lo = lo + run * C
 
         first = keep.tile([P, T], F32, name="first")
-        second_rest = keep.tile([P, T - SHARED_END], F32, name="second_rest")
-        scaled = {}
-        sums = {}
+        second_own = keep.tile([P, SHARED_START], F32, name="second_own")
+        second = keep.tile([P, T - SHARED_START], F32, name="second")
+        scaled = keep.tile([P, T - SHARED_START], F32, name="scaled")
+        turned = {}
 
-        def blocks(piece):
-            return [slice(c, c + P) for c in range(0, piece[1] - piece[0], P)]
+        def shared(tile, lo, hi):
+            return tile[:, lo - SHARED_START : hi - SHARED_START]
 
-        def pick_first(piece):
-            lo, hi = piece
+        def pick_first(lo, hi):
             nc.vector.tensor_tensor(first[:, lo:hi], y[:].indirect(pos1_sb[:, lo // 16 : hi // 16]), gate0[:, lo:hi], MULT)
 
-        def pick_second(i):
-            lo, hi = SHARED_PIECES[i]
-            second = keep.tile([P, hi - lo], F32, name=f"second{i}", tag="second", bufs=2)
-            nc.scalar.activation(second[:], y[:].indirect(pos2_sb[:, lo // 16 : hi // 16]), ACT.Copy)
-            sums[i] = psum.tile([P, hi - lo], F32, name=f"bank{i % 2}")
-            for block in blocks(SHARED_PIECES[i]):
-                nc.tensor.transpose(sums[i][:, block], second[:, block], identity[:])
-
-        def scale_second(i):
-            lo, hi = SHARED_PIECES[i]
-            scaled[i] = keep.tile([P, hi - lo], F32, name=f"scaled{i}")
-            for block in blocks(SHARED_PIECES[i]):
-                column = (lo + block.start) // P
-                nc.scalar.activation(scaled[i][:, block], sums[i][:, block], ACT.Copy, scale=gate1_columns[:, column : column + 1])
-            sums[i] = psum.tile([P, hi - lo], F32, name=f"bank{2 + i}")
-            for block in blocks(SHARED_PIECES[i]):
-                nc.tensor.transpose(sums[i][:, block], scaled[i][:, block], identity[:])
-
-        def add_and_store(piece, second):
-            lo, hi = piece
+        def add_and_store(lo, hi, other):
             total = keep.tile([P, hi - lo], F32, name=f"total{lo}")
-            nc.vector.tensor_tensor(total[:], second, first[:, lo:hi], ADD)
+            nc.vector.tensor_tensor(total[:], other, first[:, lo:hi], ADD)
             nc.sync.dma_start(out[:, lo:hi], total[:])
 
-        last = len(SHARED_PIECES) - 1
-        pick_first(FIRST_PICKS[0])
-        pick_first(FIRST_PICKS[1])
-        pick_second(0)
-        for i in range(last):
-            pick_second(i + 1)
-            scale_second(i)
-        scale_second(last)
-        add_and_store(SHARED_PIECES[0], sums[0][:])
-        pick_first(FIRST_PICKS[2])
-        add_and_store(SHARED_PIECES[1], sums[1][:])
-        nc.vector.tensor_tensor(second_rest[:], y[:].indirect(pos2_sb[:, SHARED_END // 16 : T // 16]), gate1[:], MULT)
-        for i in range(2, last + 1):
-            add_and_store(SHARED_PIECES[i], sums[i][:])
-        for lo, hi in VECTOR_ADDS:
-            add_and_store((lo, hi), second_rest[:, lo - SHARED_END : hi - SHARED_END])
+        for i, (lo, hi) in enumerate(SECOND_PICKS):
+            nc.scalar.activation(shared(second, lo, hi), y[:].indirect(pos2_sb[:, lo // 16 : hi // 16]), ACT.Copy)
+            bank = psum.tile([P, hi - lo], F32, name=f"bank{i}")
+            for t in range(lo, hi, P):
+                turned[t] = bank[:, t - lo : t - lo + P]
+                nc.tensor.transpose(turned[t], shared(second, t, t + P), identity[:])
+
+        nc.vector.tensor_tensor(second_own[:], y[:].indirect(pos2_sb[:, 0 : SHARED_START // 16]), gate1[:], MULT)
+        for lo, hi in FIRST_PICKS[:-1]:
+            pick_first(lo, hi)
+        add_and_store(0, SHARED_START, second_own[:])
+        pick_first(*FIRST_PICKS[-1])
+
+        for i, (lo, hi) in enumerate(SHARED_ADDS):
+            bank = psum.tile([P, hi - lo], F32, name=f"bank{len(SECOND_PICKS) + i}")
+            for t in range(lo, hi, P):
+                column = (t - SHARED_START) // P
+                nc.scalar.activation(shared(scaled, t, t + P), turned[t], ACT.Copy, scale=gate1_columns[:, column : column + 1])
+                nc.tensor.transpose(bank[:, t - lo : t - lo + P], shared(scaled, t, t + P), identity[:])
+            add_and_store(lo, hi, bank[:])

@@ -115,8 +115,8 @@ def tile_moe_pln_lin_gelu_kernel(
             )
         nc.sync.dma_start(pos1_sb[:], pos1)
         nc.sync.dma_start(pos2_sb[:], pos2)
-        nc.sync.dma_start(gate0[:], gate[0])
         nc.sync.dma_start(gate1[:], gate[1, :, 0:SHARED_START])
+        nc.sync.dma_start(gate0[:], gate[0])
 
         grouped = {}
         grouped_second = keep.tile([P, T, PACK], BF16, name="grouped_second", align_bytes=64)

@@ -38,7 +38,7 @@ BANK_SLOTS = tuple((lo, lo + 2 * C) for lo in range(0, 10 * C, 2 * C)) + (
     (11 * C + GROUP, 12 * C),
 )
 SHARED_START = 256
-FIRST_PICKS = ((0, 512), (512, 1024), (1024, 1536))
+FIRST_PICKS = ((0, 768), (768, 1536))
 SECOND_PICKS = ((256, 768), (768, 1280), (1280, 1536))
 SHARED_ADDS = ((256, 640), (640, 1024), (1024, 1280), (1280, 1536))
 
@@ -254,10 +254,9 @@ def tile_moe_pln_lin_gelu_kernel(
                 nc.tensor.transpose(turned[t], shared(second, t, t + P), identity[:])
 
         nc.vector.tensor_tensor(second_own[:], y[:].indirect(pos2_sb[:, 0 : SHARED_START // 16]), gate1[:], MULT)
-        for lo, hi in FIRST_PICKS[:-1]:
+        for lo, hi in FIRST_PICKS:
             pick_first(lo, hi)
         add_and_store(0, SHARED_START, second_own[:])
-        pick_first(*FIRST_PICKS[-1])
 
         for i, (lo, hi) in enumerate(SHARED_ADDS):
             bank = psum.tile([P, hi - lo], F32, name=f"bank{len(SECOND_PICKS) + i}")

@@ -38,9 +38,9 @@ BANK_SLOTS = tuple((lo, lo + 2 * C) for lo in range(0, 10 * C, 2 * C)) + (
     (11 * C + GROUP, 12 * C),
 )
 SHARED_START = 256
-FIRST_PICKS = ((0, 768), (768, 1536))
+FIRST_PICKS = ((0, 512), (512, 1024), (1024, 1536))
 SECOND_PICKS = ((256, 768), (768, 1280), (1280, 1536))
-SHARED_ADDS = ((256, 640), (640, 1024), (1024, 1280), (1280, 1536))
+SHARED_ADDS = ((256, 512), (512, 896), (896, 1280), (1280, 1536))
 
 
 def tile_moe_pln_lin_gelu_kernel(
@@ -115,6 +115,9 @@ def tile_moe_pln_lin_gelu_kernel(
             )
         nc.sync.dma_start(pos1_sb[:], pos1)
         nc.sync.dma_start(pos2_sb[:], pos2)
+        gate1_columns = small.tile([P, (T - SHARED_START) // P], F32, name="gate1_columns")
+        with nc.allow_non_contiguous_dma(reason="one value a partition"):
+            nc.sync.dma_start(gate1_columns[:], gate[1, 0, SHARED_START:T].rearrange("(c p) -> p c", p=P))
         nc.sync.dma_start(gate1[:], gate[1, :, 0:SHARED_START])
         nc.sync.dma_start(gate0[:], gate[0])
 
@@ -162,10 +165,6 @@ def tile_moe_pln_lin_gelu_kernel(
         for lo in range(0, S, HALF):
             gather(slot_words[0], x_words[0], lo, lo + HALF)
         quantise(1, grouped_second, 0, QUANTS[1])
-
-        gate1_columns = small.tile([P, (T - SHARED_START) // P], F32, name="gate1_columns")
-        with nc.allow_non_contiguous_dma(reason="one value a partition"):
-            nc.sync.dma_start(gate1_columns[:], gate[1, 0, SHARED_START:T].rearrange("(c p) -> p c", p=P))
 
         def first_pass(target, lo, hi, start):
             e = lo // C
@@ -231,7 +230,6 @@ def tile_moe_pln_lin_gelu_kernel(
 
         first = keep.tile([P, T], F32, name="first")
         second_own = keep.tile([P, SHARED_START], F32, name="second_own")
-        second = keep.tile([P, T - SHARED_START], F32, name="second")
         scaled = keep.tile([P, T - SHARED_START], F32, name="scaled")
         turned = {}
 
@@ -246,22 +244,35 @@ def tile_moe_pln_lin_gelu_kernel(
             nc.vector.tensor_tensor(total[:], other, first[:, lo:hi], ADD)
             nc.sync.dma_start(out[:, lo:hi], total[:])
 
-        for i, (lo, hi) in enumerate(SECOND_PICKS):
-            nc.scalar.activation(shared(second, lo, hi), y[:].indirect(pos2_sb[:, lo // 16 : hi // 16]), ACT.Copy)
+        def pick_second(i):
+            lo, hi = SECOND_PICKS[i]
+            second = keep.tile([P, hi - lo], F32, name=f"second{i}", tag=f"second{i % 2}")
+            nc.scalar.activation(second[:], y[:].indirect(pos2_sb[:, lo // 16 : hi // 16]), ACT.Copy)
             bank = psum.tile([P, hi - lo], F32, name=f"bank{i}")
             for t in range(lo, hi, P):
                 turned[t] = bank[:, t - lo : t - lo + P]
-                nc.tensor.transpose(turned[t], shared(second, t, t + P), identity[:])
+                nc.tensor.transpose(turned[t], second[:, t - lo : t - lo + P], identity[:])
 
-        nc.vector.tensor_tensor(second_own[:], y[:].indirect(pos2_sb[:, 0 : SHARED_START // 16]), gate1[:], MULT)
-        for lo, hi in FIRST_PICKS:
-            pick_first(lo, hi)
-        add_and_store(0, SHARED_START, second_own[:])
-
-        for i, (lo, hi) in enumerate(SHARED_ADDS):
+        def scale_and_turn_back(i):
+            lo, hi = SHARED_ADDS[i]
             bank = psum.tile([P, hi - lo], F32, name=f"bank{len(SECOND_PICKS) + i}")
             for t in range(lo, hi, P):
                 column = (t - SHARED_START) // P
                 nc.scalar.activation(shared(scaled, t, t + P), turned[t], ACT.Copy, scale=gate1_columns[:, column : column + 1])
                 nc.tensor.transpose(bank[:, t - lo : t - lo + P], shared(scaled, t, t + P), identity[:])
-            add_and_store(lo, hi, bank[:])
+            return bank
+
+        pick_second(0)
+        pick_second(1)
+        early = scale_and_turn_back(0)
+        pick_second(2)
+
+        nc.vector.tensor_tensor(second_own[:], y[:].indirect(pos2_sb[:, 0 : SHARED_START // 16]), gate1[:], MULT)
+        pick_first(*FIRST_PICKS[0])
+        pick_first(*FIRST_PICKS[1])
+        add_and_store(0, SHARED_START, second_own[:])
+        pick_first(*FIRST_PICKS[2])
+
+        add_and_store(*SHARED_ADDS[0], early[:])
+        for i in range(1, len(SHARED_ADDS)):
+            add_and_store(*SHARED_ADDS[i], scale_and_turn_back(i)[:])

@@ -39,7 +39,7 @@ BANK_SLOTS = tuple((lo, lo + 2 * C) for lo in range(0, 10 * C, 2 * C)) + (
 )
 SHARED_START = 256
 FIRST_PICKS = ((0, 512), (512, 1024), (1024, 1536))
-SECOND_PICKS = ((256, 768), (768, 1280), (1280, 1536))
+SECOND_PICKS = ((256, 512), (512, 896), (896, 1280), (1280, 1536))
 SHARED_ADDS = ((256, 512), (512, 896), (896, 1280), (1280, 1536))
 
 
@@ -246,7 +246,7 @@ def tile_moe_pln_lin_gelu_kernel(
 
         def pick_second(i):
             lo, hi = SECOND_PICKS[i]
-            second = keep.tile([P, hi - lo], F32, name=f"second{i}", tag=f"second{i % 2}")
+            second = keep.tile([P, hi - lo], F32, name=f"second{i}", tag=f"second{i % 3}")
             nc.scalar.activation(second[:], y[:].indirect(pos2_sb[:, lo // 16 : hi // 16]), ACT.Copy)
             bank = psum.tile([P, hi - lo], F32, name=f"bank{i}")
             for t in range(lo, hi, P):
@@ -264,8 +264,9 @@ def tile_moe_pln_lin_gelu_kernel(
 
         pick_second(0)
         pick_second(1)
-        early = scale_and_turn_back(0)
         pick_second(2)
+        early = scale_and_turn_back(0)
+        pick_second(3)
 
         nc.vector.tensor_tensor(second_own[:], y[:].indirect(pos2_sb[:, 0 : SHARED_START // 16]), gate1[:], MULT)
         pick_first(*FIRST_PICKS[0])

@@ -31,12 +31,9 @@ LOADS = (
 )
 QUANTS = (((512, 256), (256, 256), (256,)), (1024, 256, 256))
 SCALE_ROW = (4, 0)
-RUNS = ((8,), (2, 1, 1))
-BANK_SLOTS = tuple((lo, lo + 2 * C) for lo in range(0, 10 * C, 2 * C)) + (
-    (10 * C, 11 * C),
-    (11 * C, 11 * C + GROUP),
-    (11 * C + GROUP, 12 * C),
-)
+BYTE_RUNS = ((0, 8 * C), (8 * C, S))
+WORD_RUNS = ((0, 6 * C), (6 * C, 9 * C), (9 * C, S - 3 * GROUP), (S - 3 * GROUP, S - GROUP), (S - GROUP, S))
+BANK_SLOTS = tuple((lo, lo + 2 * C) for lo in range(0, 8 * C, 2 * C)) + ((8 * C, 9 * C),) + WORD_RUNS[2:]
 SHARED_START = 256
 FIRST_PICKS = ((0, 512), (512, 1024), (1024, 1536))
 SECOND_PICKS = ((256, 512), (512, 896), (896, 1280), (1280, 1536))
@@ -57,7 +54,7 @@ def tile_moe_pln_lin_gelu_kernel(
         pos1_sb = lists.tile([P, T // 16], U16, name="pos1_sb")
         pos2_sb = lists.tile([P, T // 16], U16, name="pos2_sb")
 
-        x_words = [keep.tile([P, (a + 1) * WINDOW], U32, name=f"x_words{a}", align_bytes=64) for a in range(2)]
+        x_words = [keep.tile([P, (2 - a) * WINDOW], U32, name=f"x_words{a}", align_bytes=64) for a in range(2)]
         x_scales = keep.tile([P, 2 * WINDOW], U8, name="x_scales", align_bytes=64)
         slot_words = [keep.tile([P, S], U32, name=f"slot_words{a}", align_bytes=64) for a in range(2)]
         slot_scales = keep.tile([P, S], U8, name="slot_scales", align_bytes=64)
@@ -74,7 +71,7 @@ def tile_moe_pln_lin_gelu_kernel(
         nc.vector.memset(x_scales[:].bitcast(I32), 0)
         make_identity(nc, identity[:])
         for a in range(2):
-            nc.vector.memset(x_words[a][:, T : (a + 1) * WINDOW].bitcast(I32), 0)
+            nc.vector.memset(x_words[a][:, T:WINDOW].bitcast(I32), 0)
         nc.vector.memset(w8_scales_sb[:].bitcast(I32), 0)
         nc.vector.memset(w4_scales_sb[:].bitcast(I32), 0)
 
@@ -192,41 +189,44 @@ def tile_moe_pln_lin_gelu_kernel(
 
         banks = {}
 
+        def expert_runs(lo, hi):
+            cuts = [lo] + [edge for edge in range(C, S, C) if lo < edge < hi] + [hi]
+            return list(zip(cuts[:-1], cuts[1:]))
+
         def open_bank(index):
             lo, hi = BANK_SLOTS[index]
             banks[index] = psum.tile([P, hi - lo], F32, name=f"bank{index}")
-            step = min(C, hi - lo)
-            for s0 in range(lo, hi, step):
-                first_pass(banks[index][:, s0 - lo : s0 - lo + step], s0, s0 + step, s0 == lo)
+            for s0, s1 in expert_runs(lo, hi):
+                first_pass(banks[index][:, s0 - lo : s1 - lo], s0, s1, s0 == lo)
 
         def close_bank(index):
             lo, hi = BANK_SLOTS[index]
-            for s0 in range(lo, hi, GROUP):
-                second_pass(banks[index][:, s0 - lo : s0 - lo + GROUP], s0, s0 + GROUP, s0 + GROUP == hi)
-            step = min(C, hi - lo)
-            for s0 in range(lo, hi, step):
+            for s0, s1 in expert_runs(lo, hi):
+                second_pass(banks[index][:, s0 - lo : s1 - lo], s0, s1, s1 == hi)
+            for s0, s1 in expert_runs(lo, hi):
                 e = s0 // C
                 nc.scalar.activation(
-                    y[:, s0 : s0 + step],
-                    banks[index][:, s0 - lo : s0 - lo + step],
-                    ACT.Gelu_apprx_tanh,
-                    bias=bias[:, e : e + 1],
+                    y[:, s0:s1], banks[index][:, s0 - lo : s1 - lo], ACT.Gelu_apprx_tanh, bias=bias[:, e : e + 1]
                 )
 
         def banks_within(lo, hi):
             return [index for index, (first, end) in enumerate(BANK_SLOTS) if lo <= first and end <= hi]
 
-        lo = 0
-        for runs in RUNS:
-            end = lo + sum(runs) * C
-            gather(slot_scales, x_scales, lo, end)
-            for index in banks_within(lo, end):
+        def gather_bytes(lo, hi):
+            gather(slot_scales, x_scales, lo, hi)
+            for index in banks_within(lo, hi):
                 open_bank(index)
-            for run in runs:
-                gather(slot_words[1], x_words[1], lo, lo + run * C)
-                for index in banks_within(lo, lo + run * C):
-                    close_bank(index)
-                lo = lo + run * C
+
+        def gather_words(lo, hi):
+            gather(slot_words[1], x_words[1], lo, hi)
+            for index in banks_within(lo, hi):
+                close_bank(index)
+
+        gather_bytes(*BYTE_RUNS[0])
+        gather_words(*WORD_RUNS[0])
+        gather_bytes(*BYTE_RUNS[1])
+        for lo, hi in WORD_RUNS[1:]:
+            gather_words(lo, hi)
 
         first = keep.tile([P, T], F32, name="first")
         second_own = keep.tile([P, SHARED_START], F32, name="second_own")

@@ -37,7 +37,7 @@ BANK_SLOTS = tuple((lo, lo + 2 * C) for lo in range(0, 8 * C, 2 * C)) + ((8 * C,
 SHARED_START = 256
 FIRST_PICKS = ((0, 512), (512, 1024), (1024, 1536))
 SECOND_PICKS = ((256, 512), (512, 896), (896, 1280), (1280, 1536))
-SHARED_ADDS = ((256, 512), (512, 896), (896, 1280), (1280, 1536))
+SHARED_ADDS = tuple((lo, lo + 256) for lo in range(SHARED_START, T, 256))
 
 
 def tile_moe_pln_lin_gelu_kernel(
@@ -255,7 +255,7 @@ def tile_moe_pln_lin_gelu_kernel(
 
         def scale_and_turn_back(i):
             lo, hi = SHARED_ADDS[i]
-            bank = psum.tile([P, hi - lo], F32, name=f"bank{len(SECOND_PICKS) + i}")
+            bank = psum.tile([P, hi - lo], F32, name=f"bank{(len(SECOND_PICKS) + i) % 8}")
             for t in range(lo, hi, P):
                 column = (t - SHARED_START) // P
                 nc.scalar.activation(shared(scaled, t, t + P), turned[t], ACT.Copy, scale=gate1_columns[:, column : column + 1])

from contextlib import ExitStack

import concourse.mybir as mybir
from concourse.masks import make_identity

K, T, E, C, N = 1024, 1536, 12, 256, 128
S = E * C
FLOPS = 2 * S * K * N

P = 128
PACK = 4
K_PASS = P * PACK
GROUP = 128
HALF = S // 2
WINDOW = 2048

F32 = mybir.dt.float32
BF16 = mybir.dt.bfloat16
I32 = mybir.dt.int32
U32 = mybir.dt.uint32
U16 = mybir.dt.uint16
U8 = mybir.dt.uint8
FP8X4 = mybir.dt.float8_e4m3fn_x4
FP4X4 = mybir.dt.float4_e2m1fn_x4
ACT = mybir.ActivationFunctionType
MULT, ADD = mybir.AluOpType.mult, mybir.AluOpType.add

LOADS = (
    ((768, 512), (512, 256), (256, 160)),
    ((512, 0), (448, 0), (320, 0), (256, 0)),
)
QUANTS = (((512, 256), (256, 256), (256,)), (1024, 256, 256))
SCALE_ROW = (4, 0)
BYTE_RUNS = ((0, 8 * C), (8 * C, S))
WORD_RUNS = ((0, 6 * C), (6 * C, 9 * C), (9 * C, S - 3 * GROUP), (S - 3 * GROUP, S - GROUP), (S - GROUP, S))
BANK_SLOTS = tuple((lo, lo + 2 * C) for lo in range(0, 8 * C, 2 * C)) + ((8 * C, 9 * C),) + WORD_RUNS[2:]
SHARED_START = 256
FIRST_PICKS = ((0, 512), (512, 1024), (1024, 1536))
SECOND_PICKS = ((256, 512), (512, 896), (896, 1280), (1280, 1536))
SHARED_ADDS = tuple((lo, lo + 256) for lo in range(SHARED_START, T, 256))


def tile_moe_pln_lin_gelu_kernel(
    tc, xT, w8_words, w8_scales, w4_words, w4_scales, b, gate, offs, pos1, pos2, out
):
    nc = tc.nc
    with ExitStack() as ctx:
        lists = ctx.enter_context(tc.tile_pool(name="lists", bufs=1))
        keep = ctx.enter_context(tc.tile_pool(name="keep", bufs=1))
        small = ctx.enter_context(tc.tile_pool(name="small", bufs=1))
        psum = ctx.enter_context(tc.psum_pool(name="psum", bufs=1))

        offs_sb = lists.tile([P, S // 16], U16, name="offs_sb")
        pos1_sb = lists.tile([P, T // 16], U16, name="pos1_sb")
        pos2_sb = lists.tile([P, T // 16], U16, name="pos2_sb")

        x_words = [keep.tile([P, (2 - a) * WINDOW], U32, name=f"x_words{a}", align_bytes=64) for a in range(2)]
        x_scales = keep.tile([P, 2 * WINDOW], U8, name="x_scales", align_bytes=64)
        slot_words = [keep.tile([P, S], U32, name=f"slot_words{a}", align_bytes=64) for a in range(2)]
        slot_scales = keep.tile([P, S], U8, name="slot_scales", align_bytes=64)
        w8_sb = keep.tile([P, E * N * 4], U8, name="w8_sb", align_bytes=64)
        w4_sb = keep.tile([P, E * N * 2], U8, name="w4_sb", align_bytes=64)
        w8_scales_sb = keep.tile([P, E * N], U8, name="w8_scales_sb", align_bytes=64)
        w4_scales_sb = keep.tile([P, E * N], U8, name="w4_scales_sb", align_bytes=64)
        bias = keep.tile([P, E], F32, name="bias")
        gate0 = keep.tile([P, T], F32, name="gate0")
        gate1 = keep.tile([P, SHARED_START], F32, name="gate1")
        y = keep.tile([P, S], F32, name="y")
        identity = keep.tile([P, P], F32, name="identity")

        nc.vector.memset(x_scales[:].bitcast(I32), 0)
        make_identity(nc, identity[:])
        for a in range(2):
            nc.vector.memset(x_words[a][:, T:WINDOW].bitcast(I32), 0)
        nc.vector.memset(w8_scales_sb[:].bitcast(I32), 0)
        nc.vector.memset(w4_scales_sb[:].bitcast(I32), 0)

        raw = {}

        def first_token(a, c):
            return sum(tokens for tokens, by_vector in LOADS[a][:c])

        def load_tokens(a, c):
            width, t0 = LOADS[a][c][0], first_token(a, c)
            raw[a, c] = keep.tile([P, PACK, width], F32, name=f"raw{a}_{c}")
            rows = xT[a * K_PASS : (a + 1) * K_PASS, t0 : t0 + width]
            nc.sync.dma_start(out=raw[a, c][:], in_=rows.rearrange("(p j) w -> p j w", j=PACK))

        for c in range(len(LOADS[0])):
            load_tokens(0, c)
        nc.sync.dma_start(offs_sb[:], offs)
        for c in range(len(LOADS[1])):
            load_tokens(1, c)

        for scales_sb, scales in ((w8_scales_sb, w8_scales), (w4_scales_sb, w4_scales)):
            for q in range(4):
                nc.sync.dma_start(
                    out=scales_sb[32 * q : 32 * q + 4, :].bitcast(I32).rearrange("r (e n) -> r e n", e=E),
                    in_=scales[:, 0, 4 * q : 4 * q + 4, :].bitcast(I32).rearrange("e r n -> r e n"),
                )
        nc.sync.dma_start(bias[:], b)
        half = E // 2
        for h in range(2):
            experts = slice(h * half, (h + 1) * half)
            nc.sync.dma_start(
                out=w4_sb[:, h * half * N * 2 : (h + 1) * half * N * 2].bitcast(I32).rearrange("p (e n) -> p e n", e=half),
                in_=w4_words[experts, 0].bitcast(I32).rearrange("e p n -> p e n"),
            )
            nc.sync.dma_start(
                out=w8_sb[:, h * half * N * 4 : (h + 1) * half * N * 4].bitcast(I32).rearrange("p (e n) -> p e n", e=half),
                in_=w8_words[experts, 0].rearrange("e p n r -> e p (n r)").bitcast(I32).rearrange("e p n -> p e n"),
            )
        nc.sync.dma_start(pos1_sb[:], pos1)
        nc.sync.dma_start(pos2_sb[:], pos2)
        gate1_columns = small.tile([P, (T - SHARED_START) // P], F32, name="gate1_columns")
        with nc.allow_non_contiguous_dma(reason="one value a partition"):
            nc.sync.dma_start(gate1_columns[:], gate[1, 0, SHARED_START:T].rearrange("(c p) -> p c", p=P))
        nc.sync.dma_start(gate1[:], gate[1, :, 0:SHARED_START])
        nc.sync.dma_start(gate0[:], gate[0])

        grouped = {}
        grouped_second = keep.tile([P, T, PACK], BF16, name="grouped_second", align_bytes=64)

        def interleave(a, c):
            width, by_vector = LOADS[a][c]
            if a == 0:
                grouped[a, c] = keep.tile([P, width, PACK], BF16, name=f"grouped{a}_{c}", align_bytes=64)[:]
            else:
                grouped[a, c] = grouped_second[:, first_token(a, c) : first_token(a, c) + width, :]

            def views(lo, hi):
                dst = grouped[a, c][:, lo:hi, :].rearrange("p (m i) j -> p m j i", i=2)
                src = raw[a, c][:, :, lo:hi].rearrange("p j (m i) -> p m j i", i=2)
                return dst, src

            if by_vector < width:
                dst, src = views(by_vector, width)
                nc.scalar.activation(dst, src, ACT.Copy)
            if by_vector > 0:
                dst, src = views(0, by_vector)
                nc.vector.tensor_copy(dst, src)

        def quantise(a, source, t0, widths):
            for call, width in enumerate(widths):
                lo = sum(widths[:call])
                hi = lo + width
                nc.vector.quantize_mx(
                    out=x_words[a][:, t0 + lo : t0 + hi].bitcast(FP8X4),
                    scales=x_scales[SCALE_ROW[a] : P, t0 + lo : t0 + hi],
                    in_=source[:, lo:hi, :].rearrange("p w j -> p (w j)"),
                )

        def gather(dst, window, lo, hi):
            columns = 2 * WINDOW if hi - lo > HALF else WINDOW
            nc.vector.tensor_copy(dst[:, lo:hi], window[:, :columns].indirect(offs_sb[:, lo // 16 : hi // 16]))

        for c in range(len(LOADS[0])):
            interleave(0, c)
            quantise(0, grouped[0, c], first_token(0, c), QUANTS[0][c])
        for c in range(len(LOADS[1])):
            interleave(1, c)
        for lo in range(0, S, HALF):
            gather(slot_words[0], x_words[0], lo, lo + HALF)
        quantise(1, grouped_second, 0, QUANTS[1])

        def first_pass(target, lo, hi, start):
            e = lo // C
            nc.tensor.matmul_mx(
                out=target,
                lhsT=w8_sb[:, e * N * 4 : (e + 1) * N * 4].bitcast(FP8X4),
                lhsT_scale=w8_scales_sb[:, e * N : (e + 1) * N],
                rhs=slot_words[0][:, lo:hi].bitcast(FP8X4),
                rhs_scale=slot_scales[SCALE_ROW[0] : P, lo:hi],
                start=start,
                stop=False,
            )

        def second_pass(target, lo, hi, stop):
            e = lo // C
            nc.tensor.matmul_mx(
                out=target,
                lhsT=w4_sb[:, e * N * 2 : (e + 1) * N * 2].bitcast(FP4X4),
                lhsT_scale=w4_scales_sb[:, e * N : (e + 1) * N],
                rhs=slot_words[1][:, lo:hi].bitcast(FP8X4),
                rhs_scale=slot_scales[SCALE_ROW[1] : P, lo:hi],
                start=False,
                stop=stop,
            )

        banks = {}

        def expert_runs(lo, hi):
            cuts = [lo] + [edge for edge in range(C, S, C) if lo < edge < hi] + [hi]
            return list(zip(cuts[:-1], cuts[1:]))

        def open_bank(index):
            lo, hi = BANK_SLOTS[index]
            banks[index] = psum.tile([P, hi - lo], F32, name=f"bank{index}")
            for s0, s1 in expert_runs(lo, hi):
                first_pass(banks[index][:, s0 - lo : s1 - lo], s0, s1, s0 == lo)

        def close_bank(index):
            lo, hi = BANK_SLOTS[index]
            for s0, s1 in expert_runs(lo, hi):
                second_pass(banks[index][:, s0 - lo : s1 - lo], s0, s1, s1 == hi)
            for s0, s1 in expert_runs(lo, hi):
                e = s0 // C
                nc.scalar.activation(
                    y[:, s0:s1], banks[index][:, s0 - lo : s1 - lo], ACT.Gelu_apprx_tanh, bias=bias[:, e : e + 1]
                )

        def banks_within(lo, hi):
            return [index for index, (first, end) in enumerate(BANK_SLOTS) if lo <= first and end <= hi]

        def gather_bytes(lo, hi):
            gather(slot_scales, x_scales, lo, hi)
            for index in banks_within(lo, hi):
                open_bank(index)

        def gather_words(lo, hi):
            gather(slot_words[1], x_words[1], lo, hi)
            for index in banks_within(lo, hi):
                close_bank(index)

        gather_bytes(*BYTE_RUNS[0])
        gather_words(*WORD_RUNS[0])
        gather_bytes(*BYTE_RUNS[1])
        for lo, hi in WORD_RUNS[1:]:
            gather_words(lo, hi)

        first = keep.tile([P, T], F32, name="first")
        second_own = keep.tile([P, SHARED_START], F32, name="second_own")
        scaled = keep.tile([P, T - SHARED_START], F32, name="scaled")
        turned = {}

        def shared(tile, lo, hi):
            return tile[:, lo - SHARED_START : hi - SHARED_START]

        def pick_first(lo, hi):
            nc.vector.tensor_tensor(first[:, lo:hi], y[:].indirect(pos1_sb[:, lo // 16 : hi // 16]), gate0[:, lo:hi], MULT)

        def add_and_store(lo, hi, other):
            total = keep.tile([P, hi - lo], F32, name=f"total{lo}")
            nc.vector.tensor_tensor(total[:], other, first[:, lo:hi], ADD)
            nc.sync.dma_start(out[:, lo:hi], total[:])

        def pick_second(i):
            lo, hi = SECOND_PICKS[i]
            second = keep.tile([P, hi - lo], F32, name=f"second{i}", tag=f"second{i % 3}")
            nc.scalar.activation(second[:], y[:].indirect(pos2_sb[:, lo // 16 : hi // 16]), ACT.Copy)
            bank = psum.tile([P, hi - lo], F32, name=f"bank{i}")
            for t in range(lo, hi, P):
                turned[t] = bank[:, t - lo : t - lo + P]
                nc.tensor.transpose(turned[t], second[:, t - lo : t - lo + P], identity[:])

        def scale_and_turn_back(i):
            lo, hi = SHARED_ADDS[i]
            bank = psum.tile([P, hi - lo], F32, name=f"bank{(len(SECOND_PICKS) + i) % 8}")
            for t in range(lo, hi, P):
                column = (t - SHARED_START) // P
                nc.scalar.activation(shared(scaled, t, t + P), turned[t], ACT.Copy, scale=gate1_columns[:, column : column + 1])
                nc.tensor.transpose(bank[:, t - lo : t - lo + P], shared(scaled, t, t + P), identity[:])
            return bank

        pick_second(0)
        pick_second(1)
        pick_second(2)
        early = scale_and_turn_back(0)
        pick_second(3)

        nc.vector.tensor_tensor(second_own[:], y[:].indirect(pos2_sb[:, 0 : SHARED_START // 16]), gate1[:], MULT)
        pick_first(*FIRST_PICKS[0])
        pick_first(*FIRST_PICKS[1])
        add_and_store(0, SHARED_START, second_own[:])
        pick_first(*FIRST_PICKS[2])

        add_and_store(*SHARED_ADDS[0], early[:])
        for i in range(1, len(SHARED_ADDS)):
            add_and_store(*SHARED_ADDS[i], scale_and_turn_back(i)[:])
